import numpy as np, ml_dtypes
CORES = [66,74,82,90,194,202,210,218]
N = 8
import mx_ref
BF = ml_dtypes.bfloat16
def pick(q, e):
    c = np.concatenate([q[0].reshape(128, -1, 4), np.zeros((128, 1, 4), np.uint8)], axis=1); s = np.concatenate([q[1], np.ones((16, 1), np.uint8)], axis=1)
    return (np.ascontiguousarray(c[:, e].reshape(128, -1)), np.ascontiguousarray(s[:, e]))
def join(*qs):
    return (np.concatenate([q[0] for q in qs], axis=1), np.concatenate([q[1] for q in qs], axis=1))
def put(q, e, v):
    c, s = q[0].reshape(128, -1, 4).copy(), q[1].copy(); c[:, e] = v[0].reshape(128, -1, 4); s[:, e] = v[1]
    return (c.reshape(128, -1), s)
def pk(c, s):
    return (np.ascontiguousarray(c), mx_ref.live(s))
def emit(q):
    return q[0], q[1]
def cols(t, e):
    v = np.concatenate([t.reshape(128, -1, 4), np.zeros((128, 1, 4), BF)], axis=1)
    return np.ascontiguousarray(v[:, e]).reshape(128, -1)
def tile(rs):
    return np.stack(rs, axis=2).reshape(128, -1).astype(BF)
def cut(t, i, w=512):
    return t[:, w * i:w * i + w]
def f(rng, *shape):
    return mx_ref.flush((rng.standard_normal(shape, dtype=np.float32) * np.exp2(rng.integers(-2, 3, shape[:-1] + (1,)))).astype(BF))
def wide(rng, *shape, cols=0):
    v = rng.standard_normal(shape, dtype=np.float32) * np.exp2(rng.integers(-12, 13, shape)).astype(np.float32)
    if cols: v *= np.repeat(np.exp2(rng.integers(-cols, cols + 1, shape[:-2] + (1, shape[-1] // 4))) * (rng.random(shape[:-2] + (1, shape[-1] // 4)) > 0.0625), 4, axis=-1).astype(np.float32)
    return mx_ref.flush(v.astype(BF))
P, K, O = 96, 32, 1
E = P + 2 * K // N
def play(x, u, a, b):
    row = mx_ref.quantize(np.concatenate([x[r] for r in range(N)], axis=1))
    num = 4 * np.arange(N * P)
    k = mx_ref.quantize(np.ascontiguousarray(u[0]))
    high = []
    for t in range(2):
        n = num.size
        s = mx_ref.matmul(k, row)[0] + np.float32(0)
        split = np.sort(np.argsort(-s, kind="stable")[:K])
        parents = pick(row, split)
        kids = []
        for m in (a[0], b[0]):
            kids.append(tile([mx_ref.matmul(mx_ref.quantize(np.ascontiguousarray(cut(m, i))), parents) * np.float32(0.0625) for i in range(4)]))
        size = np.max(np.abs(np.stack(kids).astype(np.float32)).reshape(2, 16, 8, K, 4), axis=(2, 4))
        high.append((np.max(np.abs(s)), np.max(size), np.min(np.where(size == 0, np.float32(1), size))))
        e = np.repeat(np.arange(n), 1 + np.isin(np.arange(n), split))
        first = split + np.arange(K)
        num = num[e]
        num[first + 1] += 2 - t
        e[first] = n + np.arange(K)
        e[first + 1] = n + K + np.arange(K)
        row = pick(join(row, mx_ref.quantize(kids[0]), mx_ref.quantize(kids[1])), e)
    return row, num, high
def times(t, v):
    return mx_ref.flush((t.astype(np.float32) * np.float32(v)).astype(BF))
def lift(d, r, e, v):
    s = np.where(d["u"][0][:, None, :4].astype(np.float32) < 0, -v, v)
    x = np.array(d["x"][r].astype(np.float32)).reshape(128, P, 4)
    x[:, e] = np.abs(x[:, e]) * s
    d["x"][r] = mx_ref.flush(x.reshape(128, -1).astype(BF))
def setup_inputs(rng):
    u = np.array(f(rng, 128, 512))
    u[:, 4:] = 0
    return {"x": np.array(f(rng, N, 128, 4 * P)), "u": np.stack([u] * N), "a": np.stack([f(rng, 128, 2048)] * N), "b": np.stack([f(rng, 128, 2048)] * N), "w": f(rng, N, 128, 512 * O)}
def setup_inputs_below(rng):
    d = setup_inputs(rng)
    d["x"] = np.array(times(d["x"], 2.0 ** 20))
    for r in range(N): lift(d, r, np.arange(P), -1)
    lift(d, N - 1, rng.permutation(P)[:K], -2.0 ** -6)
    v, p = d["a"][0].astype(np.float32) * np.float32(2.0 ** -6), np.arange(128)
    for i in range(4): v[p, 512 * i + 4 * p + i] = 128
    d["a"] = np.stack([mx_ref.flush(v.astype(BF))] * N)
    d["b"] = times(d["a"], 2.0 ** -4)
    return d
def setup_inputs_edge(rng):
    d = setup_inputs(rng)
    d["a"], d["b"], d["x"] = times(d["a"], 2.0 ** -12), times(d["b"], 2.0 ** -12), np.array(times(d["x"], 64))
    lift(d, int(rng.integers(1, N - 1)), rng.permutation(P)[:K], 4096)
    lift(d, N - 1, rng.permutation(P)[:K], 64)
    return d
def setup_inputs_spread(rng):
    return {**setup_inputs(rng), "x": wide(rng, N, 128, 4 * P, cols=6)}
def setup_inputs_ties(rng):
    d = setup_inputs(rng)
    v, e = times(f(rng, 128, 24), 2.0 ** 14), (rng.permutation(N * P) % 6).reshape(N, P)
    d["x"] = np.stack([cols(v, e[r]) for r in range(N)])
    lift(d, N - 1, rng.permutation(P)[:K // 8], 64)
    return {**d, "b": d["a"].copy()}
def setup_inputs_zero(rng):
    d = setup_inputs(rng)
    d["u"][:, 64:] = 0
    for r in range(N):
        kind = rng.permutation(P) % 3
        lift(d, r, np.flatnonzero(kind == 2), -1)
        x = np.array(d["x"][r]).reshape(128, P, 4)
        x[:, kind == 0] = 0
        x[:64, kind == 1] = 0
        d["x"][r] = x.reshape(128, -1)
    return d
def check_inputs(d):
    b = []
    for k in ("x", "u", "a", "b", "w"):
        v = np.abs(d[k].astype(np.float32))
        if not (np.isfinite(v).all() and ((v == 0) | (v >= 2.0 ** -30) & (v <= 2.0 ** 30)).all()): b.append("a value of " + k)
    if (d["u"][:, :, 4:].astype(np.float32) != 0).any(): b.append("u has numbers behind its column 0")
    for k in ("u", "a", "b"):
        v = d[k].astype(np.float32)
        if (v != v[:1]).any(): b.append(k + " differs between ranks")
    if not b:
        try:
            high = play(d["x"], d["u"], d["a"], d["b"])[2]
            if not all(np.isfinite(s) for s, c, m in high): b.append("a score")
            if not all(c <= 2.0 ** 30 and m >= 2.0 ** -30 for s, c, m in high): b.append("a number of a child")
        except Exception:
            b.append("a number of a child")
    return b
def reference(x, u, a, b, w):
    row, num, _ = play(x, u, a, b)
    oc, osc = np.zeros((N, 128, 4 * E), np.uint8), np.zeros((N, 16, E), np.uint8)
    hs, y = np.zeros((N, 1, E), np.float32), np.zeros((N, 128, O * E), np.float32)
    for r in range(N):
        q = pick(row, np.arange(r * E, r * E + E))
        oc[r], osc[r] = emit(q)
        hs[r, 0] = num[r * E:r * E + E]
        for o in range(O):
            y[r, :, o * E:o * E + E] = mx_ref.matmul(mx_ref.quantize(np.ascontiguousarray(cut(w[r], o))), q)
    return {"oc": oc, "osc": osc, "hs": hs, "y": y}

@@ -1,0 +1,642 @@
+from concourse.bass import DstId, RemoteDMATransfer
+from concourse.mybir import dt, AluOpType, AxisListType, ActivationFunctionType
+
+N, P, K = 8, 96, 32
+E = P + 2 * K // N
+AA, AB, BA, BB = 6, 7, 11, 12
+H0 = 3 * P
+HN = 72
+ALL = H0 + BB * P + HN
+UNIT = 2.0 ** -20
+HUGE = 1.0e29
+CODE = "float8_e4m3fn_x4"
+HALF = "bfloat16"
+CYCLE, SYNC, OWN, FLY, LOCAL = 0.0009, 0.16, 0.14, 1.6, 2.0
+ORDER = """
+load.u:s XT.0.384:v load.x:y Z32.0.0:v U0.0.8:v load.a:y KAP.3.0:s PI.0.0:q PM.0.1:v KAP.0.0:s VR.3.0:v THR.2.0:s ZB.0.0:v
+PF.0.0:v PM.0.0:v X16.0.0:v WC.1.2:s load.b:s X32.0.0:v PA.0.0:v QV.0.0:v load.w:y KAP.1.0:s WC.1.0:s SRC.0.0:v WC.1.1:s
+HK.0.288:v FI.0.0:q UT.0.3:v UT.0.1:v WC.2.3:s WC.3.2:s JC.0.0:s ps.0.0:p X1S.0.0:s KAP.2.0:s UT.0.0:v UT.0.2:v XA.0.0:v
+WC.0.0:s XB.0.0:v QU.0.0:v XB.0.2:v PB.0.0:v H2.0.0:s X2L.0.2:v ps.0.512:p XB.0.1:v SROW.0.0:s KV.0.0:v send.x1:q PC.0.0:v
+FC.1.0:s WC.1.3:s WC.2.2:s SQ.0.0:s PC.0.1:v WC.3.1:s TS.0.0:v THR.0.0:s WH.0.128:s WC.3.3:s JC.2.0:v codes.1:q WC.0.2:s
+SQ.2.0:s scales.1:q TRI.0.32:v QA.0.0:v QB.0.0:v WC.0.1:s SQ.3.0:v WC.3.0:s SQ.1.0:s ps.0.1024:p WC.2.1:s KT.0.2:s ps.0.1536:p
+OE.0.32:v OE.0.64:v ps.0.0.2:p VR.2.0:s ps.0.3584:p ps.0.3072:p FC.2.0:s KT.0.3:s WC.0.3:s TRI.0.64:v FC.3.0:s CM.0.512:v
+W.0.256:s codes.0:q OE.0.0:v CM.0.544:v TRI.0.0:v KT.0.0:v come.x1:- WC.2.4:s KT.0.387:s CM.0.800:v CM.0.224:v ps.0.2560:p
+CM.0.832:v CM.0.256:v EX1.0.192:v NS.0.0:s EX1.0.64:s ps.0.2048:p EX1.0.32:v EX1.0.96:s KT.0.386:s P2.0.0:s EX1.0.160:v
+ps.0.512.2:p FC.0.0:s KT.0.385:s EX1.0.0:v KT.0.384:s EX1.0.128:v KT.0.1:s R1.0.0:v WC.2.8:s CN.0.288:v GE.0:v GE.1:v
+scales.0:q SRC.0.96:v TG.0.0:s TA.1:s TA.0:s GT.0:v W.0.260:s WC.2.0:s GT.1:v NH.0.0:s CN.0.0:v WC.0.4:s CN.0.144:v E0.0.0:s
+CN.0.431:v CA.0.0:v CA.1.3:v CA.0.3:v ps.0.0.3:p CA.1.0:v E0.0.32:s PN.0.0:s WC.3.8:s THR.1.0:s E0.0.64:v VR.0.0:s EX3.0.0:v
+VR.1.0:s EX3.0.64:v EX3.0.32:v PR.2.0:v PR.0.0:v OH.0.0:v come.halo:- THR.3.0:s M2.0.0:v M1.0.0:v ps.0.2048.2:p ps.0.512.3:p
+XS.0.0:v ps.0.1536.2:p XS.0.1:s HK.0.2:v ps.0.3584.2:p WC.0.8:v HK.0.0:s X2L.0.0:s HK.0.386:s HK.0.3:v ps.0.1024.2:p
+ps.0.3072.2:p ps.0.2560.2:p GO.0.2:s WC.1.8:s NN.0.0:s ps.0.0.4:p send.x2:q HK.0.1:v GO.0.0:s HK.0.385:s GO.0.1:v GO.0.3:s
+QW.0.0:v HK.0.384:s GO.0.769:s GO.0.770:v SRC.0.576:v come.x2:- HK.0.387:v SRC.0.384:v SC.0.0:s SC.0.1:s GO.0.771:v EX2.0.32:v
+EX2.2.32:s EX2.0.0:s EX2.2.96:s EX2.0.96:v EX2.0.64:s DS.0.0:v GO.0.768:s ps.0.1536.3:p DS.1.64:s ps.0.3072.3:p DS.3.64:s
+DN.0.0:v ps.0.2048.3:p DS.0.64:v DN.0.64:s ps.0.1024.3:p DN.3.64:s DS.2.64:v SG.0.0:s DN.1.64:v DN.2.64:v SRC.0.1056:v LO.0.0:v
+ps.0.512.4:p HG.0.2:s HG.0.3:s HG.0.1:s BF.0.0:v P1.0.0:v HG.0.673:s HG.0.0:s EXM.0.0:v MR.0.0:v ps.0.2560.3:p MR.2.32:v
+HG.0.672:s MR.0.32:v F0.0.0:v MR.3.64:v MR.1.64:v F32.0.0:v MR.2.64:s ps.0.3584.3:p MR.0.64:s ps.0.0.5:p HG.0.674:s sg.RK.0:s
+EXF.2.32:s EXF.0.32:s SRC.0.864:v HG.0.675:v EXF.0.0:s SRC.0.1344:v FR.0.0:v FR.2.64:v FR.0.64:v sg.SB.1:s sg.SB.0:s FR.3.64:s
+FR.1.64:s W.0.32:v high:v low:v W.0.0:v W.0.264:v AB.0.0:s W.0.360:v sg.W.257:s W.0.392:s W.0.192:v W.0.96:v W.0.160:v
+W.0.224:v W.0.64:v W.0.128:v W.0.328:v sg.W.521:s W.0.488:s W.0.424:s W.0.296:v OF.0.0:v W.0.456:s OF.0.130:v WH.0.0:v
+OTF.2.6:v OTF.0.0:s OTF.2.0:v OTF.2.4:s OTF.0.2:v OTF.0.6:s OTF.1.4:v OTF.1.6:s OTF.2.2:s OTF.3.0:s OTF.0.4:v OTF.1.2:v
+OTF.3.4:v OTF.1.0:s OTF.3.2:v OTF.3.6:v OT.0.0:v sg.WH.129:s sRUN.0.0:s sg.WH.130:s RUN.0.0:v WH.0.64:v WH.0.96:v WH.0.32:v
+store.o2:y ps.0.0.6:p store.o4:s store.o3:y store.o1:y HB.0.0:s YT.0.0:s store.o5:s store.o0:y store.o6:y
+"""
+
+
+def _sb(n, d="float32"):
+    return ("sbuf", [128, n], d)
+
+
+SCRATCH = {
+    "XT": _sb(512, HALF), "U0": _sb(512, HALF), "UT": _sb(512, HALF), "ZB": _sb(128, HALF),
+    "AT": _sb(2048, HALF), "BT": _sb(2048, HALF), "WT": _sb(512, HALF),
+    "QU": _sb(128, CODE), "sQU": _sb(128, "uint8"), "QV": _sb(128, CODE), "sQV": _sb(128, "uint8"),
+    "QA": _sb(512, CODE), "sQA": _sb(512, "uint8"), "QB": _sb(512, CODE), "sQB": _sb(512, "uint8"),
+    "QW": _sb(128, CODE), "sQW": _sb(128, "uint8"),
+    "SRC": _sb(ALL, CODE), "sSRC": _sb(ALL, "uint8"),
+    "KT": _sb(768, HALF), "GO": _sb(1536, HALF), "HK": _sb(672, HALF), "HG": _sb(1344, HALF),
+    "RUN": _sb(128, CODE), "sRUN": _sb(128, "uint8"), "YT": _sb(E),
+    "ps": ("psum", [128, 4096], "float32"),
+    "Z32": _sb(32), "PI": _sb(1, "int32"), "PM": _sb(2, "int32"), "PF": _sb(1), "X32": _sb(1), "X16": _sb(1),
+    "FI": _sb(96), "XA": _sb(1), "XB": _sb(3), "TRI": _sb(96), "JC": _sb(1), "KAP": _sb(1), "KV": _sb(96), "VR": _sb(96), "FC": _sb(1),
+    "PA": _sb(1), "PB": _sb(1), "PC": _sb(2), "P2": _sb(2), "PN": _sb(2), "NN": _sb(1), "NS": _sb(2), "H2": _sb(1), "NH": _sb(1),
+    "WC": _sb(16), "THR": _sb(32),
+    "X1S": _sb(1), "X1L": _sb(7), "SROW": _sb(96), "SQ": _sb(32), "TS": _sb(96), "OE": _sb(96),
+    "EX1": _sb(224), "R1": _sb(224), "CM": _sb(864, HALF), "CN": _sb(432, HALF), "CA": _sb(6), "TG": _sb(224, HALF), "TA": _sb(2),
+    "E0": _sb(96), "EX3": _sb(96), "PR": _sb(96), "OH": _sb(96), "M1": _sb(96), "M2": _sb(96),
+    "XS": _sb(2), "X2L": _sb(20), "SC": _sb(2), "EX2": _sb(128), "DS": _sb(128), "DN": _sb(128), "SG": _sb(128, HALF), "LO": _sb(128, HALF),
+    "BF": _sb(128, HALF), "P1": _sb(64), "EXM": _sb(32), "MR": _sb(128),
+    "F0": _sb(1), "F32": _sb(32), "RK": _sb(1), "SB": _sb(2), "EXF": _sb(64), "FR": _sb(128), "J4": _sb(2304),
+    "W": _sb(528), "AB": _sb(128), "OF": _sb(260), "OTF": _sb(8), "OT": _sb(8, "uint16"),
+    "WH": _sb(132), "HB": _sb(1),
+}
+COUNTERS = ["v", "s", "p", "q"]
+DMAS = ["dx", "du", "da", "db", "dw", "w2", "w3", "o0", "o1", "o2", "o3", "o4", "o5", "o6"]
+SEMAPHORES = COUNTERS + DMAS + ["x1", "x2", "halo", "left"]
+AF = ActivationFunctionType
+ADD, SUB, MUL, MIN, MAX = AluOpType.add, AluOpType.subtract, AluOpType.mult, AluOpType.min, AluOpType.max
+GT, GE, LT, LE, EQ = AluOpType.is_gt, AluOpType.is_ge, AluOpType.is_lt, AluOpType.is_le, AluOpType.is_equal
+
+
+def view(name, c0=0, c1=None, p0=0, p1=128, step=1):
+    if c1 is None:
+        c1 = SCRATCH[name][1][1]
+    return (name, p0, p1, c0, c1, step)
+
+
+def quarter(name, a, c0=0, c1=None, step=1):
+    return view(name, c0, c1, 32 * a, 32 * a + 32, step)
+
+
+def half(name, h, c0=0, c1=None):
+    return view(name, c0, c1, 64 * h, 64 * h + 64)
+
+
+def width(w):
+    return len(range(w[3], w[4], w[5]))
+
+
+def meet(a, b):
+    if a[1] >= b[2] or b[1] >= a[2] or a[3] >= b[4] or b[3] >= a[4]:
+        return False
+    if a[5] == 1 and b[5] == 1:
+        return True
+    return bool(set(range(a[3], a[4], a[5])) & set(range(b[3], b[4], b[5])))
+
+
+def holds(a, b):
+    return a[5] == 1 and a[1] <= b[1] and a[2] >= b[2] and a[3] <= b[3] and a[4] >= b[4]
+
+
+def wide(w):
+    if w[0] != "ps":
+        return w
+    return ("ps", 0, 128, w[3] // 512 * 512, (w[4] + 511) // 512 * 512, 1)
+
+
+def accesses(o):
+    return [(w, False) for w in o["rd"]] + [(w, True) for w in o["wr"]]
+
+
+def links(ops):
+    n, log = len(ops), {}
+    before = [dict() for _ in ops]
+    last = None
+    for i, o in enumerate(ops):
+        for w, wr in accesses(o):
+            for v, vr, j in log.get(w[0], []):
+                if j != i and (wr or vr or w[0] == "ps") and meet(wide(w), v):
+                    before[i].setdefault(j, 0.0)
+        if "behind" in o:
+            before[i][o["behind"]] = 0.0
+        if o["qs"] == "q":
+            if last is not None:
+                before[i].setdefault(last, -ops[last]["lag"])
+            last = i
+        for w, wr in accesses(o):
+            w = wide(w)
+            l = log.setdefault(w[0], [])
+            if wr:
+                l[:] = [e for e in l if e[2] == i or not holds(w, e[0])]
+            l.append((w, wr, i))
+    keys, seen = [], {}
+    for o in ops:
+        w = (o["wr"] or o["rd"])[0]
+        k = o.get("key") or "%s.%d.%d" % (w[0], w[1] // 32, w[3])
+        seen[k] = seen.get(k, 0) + 1
+        keys.append(k if seen[k] == 1 else "%s.%d" % (k, seen[k]))
+    return before, keys
+
+
+def place(ops, before, keys, table):
+    n = len(ops)
+    after = [[] for _ in ops]
+    for i in range(n):
+        for j in before[i]:
+            after[j].append(i)
+    missing = [len(b) for b in before]
+    ready = [i for i in range(n) if missing[i] == 0]
+    queue = [""] * n
+    if table:
+        rank = {}
+        for k, x in enumerate(table.split()):
+            x = x.split(":")
+            rank[x[0]] = (float(k), x[1])
+        at, order = [0.0] * n, []
+        for i in range(n):
+            at[i], queue[i] = rank.get(keys[i], (max([at[j] for j in before[i]], default=0.0) + 0.5, ops[i]["qs"][:1] or "-"))
+        while ready:
+            i = min(ready, key=lambda k: (at[k], k))
+            ready.remove(i)
+            order.append(i)
+            for k in after[i]:
+                missing[k] -= 1
+                if missing[k] == 0:
+                    ready.append(k)
+        return order, queue
+    way = [0.0] * n
+    for i in reversed(range(n)):
+        o = ops[i]
+        way[i] = o["cost"] + o["lag"] + max([way[k] + before[k][i] + OWN for k in after[i]], default=0.0)
+    busy = {}
+    start, end = [0.0] * n, [0.0] * n
+    while ready:
+        i = max(ready, key=lambda k: (way[k], -k))
+        ready.remove(i)
+        o, best = ops[i], None
+        for q in o["qs"] or ["-"]:
+            t = 0.0
+            for j, gap in before[i].items():
+                wake = 0.0 if q == "-" else SYNC if queue[j] != q else OWN if q in "vs" else 0.0
+                t = max(t, end[j] + gap + wake)
+            if q != "-":
+                for s, e in busy.setdefault(q, []):
+                    if t + o["cost"] <= s + 1e-9:
+                        break
+                    t = max(t, e)
+            if best is None or t < best[0] - 1e-9:
+                best = (t, q)
+        start[i], queue[i] = best
+        end[i] = start[i] + o["cost"] + o["lag"]
+        if queue[i] != "-":
+            busy[queue[i]] = sorted(busy[queue[i]] + [(start[i], start[i] + o["cost"])])
+        for k in after[i]:
+            missing[k] -= 1
+            if missing[k] == 0:
+                ready.append(k)
+    return sorted(range(n), key=lambda i: (start[i], i)), queue
+
+
+def rank_program(g, core, T, topo):
+    r = T.rank_of(core)
+    if r is None:
+        return
+    queues = {"v": g.vector, "s": g.scalar, "p": g.tensor, "q": g, "y": g.sync}
+    ops = []
+
+    def ap(w):
+        n, p0, p1, c0, c1, st = w
+        return T[n][p0:p1, c0:c1] if st == 1 else T[n][p0:p1, c0:c1:st]
+
+    def op(qs, fn, reads, writes, cost, sem=None, inc=1, local=True, lag=0.0):
+        ops.append({"qs": qs, "fn": fn, "rd": reads, "wr": writes, "cost": cost, "sem": sem, "inc": inc, "local": local, "lag": lag})
+
+    def named(key):
+        ops[-1]["key"] = key
+
+    def val(x):
+        return ap(x) if isinstance(x, tuple) else x
+
+    def time(n, *sides):
+        if sides and all(SCRATCH[w[0]][2] == HALF for w in sides):
+            n = n / 2
+        return max(64, n) * CYCLE
+
+    def act(o, i, func=AF.Copy, bias=None, scale=None, acc=None):
+        kw = {}
+        for k, x in (("bias", bias), ("scale", scale), ("accum_out", acc)):
+            if x is not None:
+                kw[k] = val(x)
+        op("s", lambda e, q: e.activation(ap(o), ap(i), func, **kw), [i] + [x for x in (bias, scale) if isinstance(x, tuple)],
+           [o] + ([acc] if acc is not None else []), time(width(i)) + (0.025 if acc is not None else 0.0))
+
+    def ts(o, i, s1, op0, s2=None, op1=None):
+        rd = [i] + [s for s in (s1, s2) if isinstance(s, tuple)]
+        if op1 is None:
+            op("v", lambda e, q: e.tensor_scalar(ap(o), ap(i), val(s1), None, op0), rd, [o], time(width(i), o, i))
+        else:
+            op("v", lambda e, q: e.tensor_scalar(ap(o), ap(i), val(s1), val(s2), op0, op1), rd, [o], time(width(i), o, i))
+
+    def copy(o, i, scale=None, qs="vs"):
+        def fn(e, q):
+            if q == "v":
+                return e.tensor_copy(ap(o), ap(i)) if scale is None else e.tensor_scalar(ap(o), ap(i), scale, None, MUL)
+            return e.activation(ap(o), ap(i), AF.Copy) if scale is None else e.activation(ap(o), ap(i), AF.Copy, scale=scale)
+        op(qs, fn, [i], [o], time(width(i)))
+
+    def spread(o, x, z=None):
+        z = z or view("Z32", 0, 32, x[1], x[2])
+
+        def fn(e, q):
+            if q == "v":
+                return e.tensor_scalar(ap(o), ap(z), ap(x), None, ADD)
+            return e.activation(ap(o), ap(z), AF.Identity, bias=ap(x))
+        op("vs", fn, [z, x], [o], time(32))
+
+    junk = [0]
+
+    def waste(i):
+        junk[0] += width(i)
+        return view("J4", junk[0] - width(i), junk[0], i[1], i[2])
+
+    def sums(o, i):
+        j = waste(i)
+
+        def fn(e, q):
+            if q == "v":
+                return e.tensor_reduce(ap(o), ap(i), AxisListType.X, ADD)
+            return e.activation(ap(j), ap(i), AF.Copy, accum_out=ap(o))
+        op("vs", fn, [i], [o, j], time(width(i)) + 0.01)
+
+    def count(name, c0, i, first=0.0):
+        n, p0, p1, a, b, _ = i
+        m = (a + b) // 2
+        o, x, y = view(name, c0, c0 + m - a, p0, p1), view(n, a, m, p0, p1), view(n, m, b, p0, p1)
+        op("v", lambda e, q: e.tensor_tensor_scan(ap(o), ap(x), ap(y), first, ADD, ADD), [x, y], [o], time(m - a, o, x))
+
+    def signs(i, bias, acc, scale=1.0):
+        act(waste(i), i, AF.Sign, bias=bias, scale=scale, acc=acc)
+        named("sg.%s.%d" % (acc[0], acc[3]))
+
+    def tt(o, a, b, o0):
+        op("v", lambda e, q: e.tensor_tensor(ap(o), ap(a), ap(b), o0), [a, b], [o], time(2 * width(a)))
+
+    def fill(o, c):
+        op("v", lambda e, q: e.memset(ap(o), c), [], [o], time(width(o), o))
+
+    def turn(o, i):
+        op("v", lambda e, q: e.transpose(ap(o), ap(i)), [i], [o], time(width(i)))
+
+    def swap(name, n, both=False):
+        if both:
+            for h in (0, 1):
+                copy(half(name, h, n, 2 * n), half(name, 1 - h, 0, n))
+        for a in range(4):
+            copy(quarter(name, a, 2 * n, 4 * n), quarter(name, a ^ 1, 0, 2 * n))
+
+    def quant(dst, c0, n, src, e0=0):
+        o, s, i = view(dst, c0, c0 + n), view("s" + dst, c0, c0 + n), view(src, e0, e0 + 4 * n)
+        op("v", lambda e, q: e.quantize_mx(ap(o), ap(s), ap(i)), [i], [o, s], 0.015 + 0.001 * n)
+
+    def mm(bk, w, wc, x, xc, n):
+        o = view("ps", 512 * bk, 512 * bk + n)
+        a, sa, b, sb = view(w, wc, wc + 128), view("s" + w, wc, wc + 128), view(x, xc, xc + n), view("s" + x, xc, xc + n)
+        op("p", lambda e, q: e.matmul_mx(ap(o), ap(a), ap(sa), ap(b), ap(sb), True, True), [a, sa, b, sb], [o], 1.3 * CYCLE * (n + 16))
+
+    def bank(i, n, p0=0, p1=128, c0=0):
+        return view("ps", 512 * i + c0, 512 * i + c0 + n, p0, p1)
+
+    def load(q, name, dst, n, sem, more=0.0):
+        o = view(dst, 0, n)
+        op(q, lambda e, q: e.dma_start(ap(o), T[name][:, 0:n]), [], [o], 0.06, sem, 16, lag=LOCAL + more)
+        named("load." + name)
+
+    def store(fn, i, sem):
+        op("ys", lambda e, q: fn(e), [i], [], 0.06, sem, 16, lag=LOCAL)
+        named("store." + sem)
+
+    def move(q, dst, d0, src, s0, n, s1, s2):
+        o, i, os, is_ = view(dst, d0, d0 + n), view(src, s0, s0 + n), view("s" + dst, d0, d0 + n), view("s" + src, s0, s0 + n)
+        op(q, lambda e, q: e.dma_start(ap(o).bitcast(dt.uint8), ap(i).bitcast(dt.uint8)), [i], [o], 0.06, s1, 16, lag=LOCAL)
+        named(s1)
+        op(q, lambda e, q: e.dma_start(ap(os), ap(is_)), [is_], [os], 0.06, s2, 16, lag=LOCAL)
+        named(s2)
+
+    others = [d for d in range(N) if d != r]
+    where = [topo.addr(T.cores[d], core) for d in others]
+    mask = topo.mask(core, T.cores[others[0]])
+    for d in others:
+        mask &= topo.mask(core, T.cores[d])
+    lanes = bin(mask).count("1")
+
+    def to_all(src, land, c0, k, sem):
+        dsts = []
+        for d in others:
+            j = r if r < d else r - 1
+            dsts.append(T[land][:, c0 + k * j:c0 + k * j + k])
+        tr = RemoteDMATransfer(dst_ids=[DstId(rid=int(a), pnc=int(b)) for a, b in where], dma_engine_mask=mask,
+                               remote_sem=T.sem[sem], srcs=[ap(src)], dsts=dsts, alu_op=0)
+        op("q", lambda e, q: e.remote_dma_fused([tr], local_sem=T.sem.left), [src], [], 1.0, "left", lanes, False, FLY)
+        named("send." + sem)
+
+    def to_one(d, d0, s0, n):
+        rid, pid = topo.addr(T.cores[d], core)
+        m = topo.mask(core, T.cores[d])
+        ln = bin(m).count("1")
+        c, s = view("SRC", s0, s0 + n), view("sSRC", s0, s0 + n)
+        oc, os = T.SRC[:, d0:d0 + n].bitcast(dt.uint8), T.sSRC[:, d0:d0 + n]
+        op("q", lambda e, q: e.remote_dma(oc, ap(c).bitcast(dt.uint8), T.sem.halo, T.sem.left, pid, rid, m), [c], [], 0.7, "left", ln, False, FLY)
+        named("codes.%d" % (d > r))
+        op("q", lambda e, q: e.remote_dma(os, ap(s), T.sem.halo, T.sem.left, pid, rid, m), [s], [], 0.7, "left", ln, False, FLY)
+        named("scales.%d" % (d > r))
+
+    def arrive(sem, n, writes):
+        ops.append({"qs": "", "fn": None, "rd": [], "wr": writes, "cost": 0.0, "sem": sem, "inc": n, "local": False, "lag": 0.0,
+                    "behind": max(k for k, o in enumerate(ops) if o["sem"] == "left"), "key": "come." + sem})
+
+    load("s", "u", "U0", 8, "du")
+    load("y", "x", "XT", 4 * P, "dx", 0.0)
+    load("y", "a", "AT", 2048, "da", 2.0)
+    load("s", "b", "BT", 2048, "db", 2.0)
+    load("y", "w", "WT", 512, "dw", 2.0)
+    op("q", lambda e, q: e.iota(T.PI[:], [[0, 1]], 0, 1), [], [view("PI")], 0.16)
+    op("q", lambda e, q: e.iota(T.FI[:], [[1, 96]], 0, 0, allow_small_or_imprecise_dtypes=True), [], [view("FI")], 0.37)
+    fill(view("Z32"), 0.0)
+    fill(view("ZB"), 0.0)
+    fill(view("U0", 8, 512), 0.0)
+    fill(view("XT", 4 * P, 512), 0.0)
+    op("v", lambda e, q: e.tensor_scalar(T.PM[:, 0:1], T.PI[:], 31, None, AluOpType.bitwise_and), [view("PI")], [view("PM", 0, 1)], time(1))
+    op("v", lambda e, q: e.tensor_scalar(T.PM[:, 1:2], T.PI[:], 15, None, AluOpType.bitwise_and), [view("PI")], [view("PM", 1, 2)], time(1))
+    copy(view("PF"), view("PI"), qs="v")
+    copy(view("X32"), view("PM", 0, 1), qs="v")
+    copy(view("X16"), view("PM", 1, 2), qs="v")
+    tt(view("PA"), view("PF"), view("X32"), SUB)
+    tt(view("XA"), view("X32"), view("PA"), SUB)
+    tt(view("PB"), view("PA"), view("X16"), ADD)
+    alpha, beta, sigma = (BA - 1, BB, 2, 2), (AA, AB - 2, 1, 1), (1, 3, 1, 2)
+    for a in range(4):
+        for buf, c, v in (("KAP", 0, (4.0 * P * r + sigma[a]) * UNIT), ("FC", 0, 2.0 - 0.5 * sigma[a] + 127.0), ("WC", 0, 2.0 * P * alpha[a]),
+                          ("WC", 1, 2.0 * P * beta[a]), ("WC", 2, float(sigma[a])), ("WC", 3, -2.0 * P * beta[a])):
+            act(quarter(buf, a, c, c + 1), quarter("Z32", a, 0, 1), bias=v)
+        act(quarter("THR", a), quarter("Z32", a), bias=0.5 - K if a < 3 else -1000.0)
+    quant("QV", 0, 128, "U0")
+    quant("SRC", 0, 128, "XT")
+
+    mm(0, "SRC", 0, "QV", 0, 128)
+    copy(view("X1S"), bank(0, 1))
+    for t in range(4):
+        ts(view("UT", t, 512, step=4), view("ZB"), view("U0", t, t + 1), ADD)
+    quant("QU", 0, 128, "UT")
+    mm(1, "QU", 0, "SRC", 0, 128)
+    copy(view("SROW"), bank(1, 96))
+    to_all(view("X1S"), "X1L", 0, 1, "x1")
+    arrive("x1", 7 * lanes, [view("X1L")])
+    if r < N - 1:
+        to_one(r + 1, H0, P - (56 - 8 * r), 56 - 8 * r)
+    if r > 0:
+        to_one(r - 1, H0 + HN - 8 * r, 0, 8 * r)
+    land, cnt = [], 0
+    if r > 0:
+        land += [view("SRC", H0, H0 + 64 - 8 * r), view("sSRC", H0, H0 + 64 - 8 * r)]
+        cnt += 2 * bin(topo.mask(T.cores[r - 1], core)).count("1")
+    if r < N - 1:
+        land += [view("SRC", H0 + 64 - 8 * r, H0 + HN), view("sSRC", H0 + 64 - 8 * r, H0 + HN)]
+        cnt += 2 * bin(topo.mask(T.cores[r + 1], core)).count("1")
+    arrive("halo", cnt, land)
+    if r == 0:
+        move("y", "SRC", H0, "SRC", 0, 64, "w2", "w3")
+    if r == N - 1:
+        move("y", "SRC", H0 + 8, "SRC", 0, 64, "w2", "w3")
+
+    turn(view("TS"), view("SROW"))
+    for a in range(4):
+        copy(quarter("SQ", a), quarter("SROW", a, 32 * (a % 3), 32 * (a % 3) + 32))
+    quant("QA", 0, 512, "AT")
+    for i in range(4):
+        mm(i, "QA", 128 * i, "SRC", 0, 128)
+    quant("QB", 0, 512, "BT")
+    for i in range(4):
+        mm(4 + i, "QB", 128 * i, "SRC", 0, 128)
+    for i in range(8):
+        copy(view("KT", i % 4 + 384 * (i // 4), 384 + 384 * (i // 4), step=4), bank(i, 96), 0.0625)
+    for b in range(3):
+        ts(view("XB", b, b + 1), view("XA"), 32.0 * b, ADD)
+    for b in range(3):
+        s, o = view("TS", 32 * b, 32 * b + 1), 288 * b
+        ts(view("TRI", 32 * b, 32 * b + 32), view("FI", 0, 32), view("XB", b, b + 1), LT)
+        ts(view("OE", 32 * b, 32 * b + 32), view("SQ"), s, EQ)
+        ts(view("CM", o + 224, o + 256), view("SQ"), s, GT)
+        tt(view("CM", o + 256, o + 288), view("OE", 32 * b, 32 * b + 32), view("TRI", 32 * b, 32 * b + 32), MUL)
+    count("CN", 288, view("CM", 800, 864), 32.0 * r)
+    copy(view("JC"), view("X32"))
+    ts(quarter("JC", 2), quarter("X32", 2), 32.0, ADD)
+    ts(view("KV"), view("FI"), 4.0 * UNIT, MUL, view("KAP"), ADD)
+    fill(quarter("VR", 3), -HUGE)
+    copy(quarter("VR", 2), quarter("SROW", 2))
+    quant("SRC", P, 2 * P, "KT")
+    mm(0, "QU", 0, "SRC", P, 2 * P)
+    copy(quarter("VR", 0), bank(0, 96, 0, 32))
+    copy(quarter("VR", 1), bank(0, 96, 32, 64, 96))
+
+    for i in range(4):
+        mm(1 + i, "QA", 128 * i, "SRC", P, 2 * P + HN)
+    for i in range(4):
+        mm((5 + i) % 8, "QB", 128 * i, "SRC", P, 2 * P + HN)
+    fill(view("HK", 4 * HN, 4 * P), 0.0)
+    for i in range(8):
+        e0 = 4 * P * (i // 4)
+        copy(view("HK", e0 + i % 4, e0 + 4 * HN, step=4), bank((1 + i) % 8, HN, c0=2 * P), 0.0625)
+    for i in range(8):
+        e0 = 768 * (i // 4)
+        copy(view("GO", e0 + i % 4, e0 + 768, step=4), bank((1 + i) % 8, 2 * P), 0.0625)
+    quant("SRC", H0 + P, P + HN, "HK")
+
+    for j in range(N - 1):
+        spread(view("EX1", 32 * j, 32 * j + 32), view("X1L", j, j + 1))
+    turn(view("R1"), view("EX1"))
+    for b in range(2):
+        s, o = view("TS", 32 * b, 32 * b + 1), 288 * b
+        if r > 0:
+            ts(view("CM", o, o + 32 * r), view("R1", 0, 32 * r), s, GE)
+            named("GE.%d" % b)
+        if r < N - 1:
+            ts(view("CM", o + 32 * r, o + 224), view("R1", 32 * r, 224), s, GT)
+            named("GT.%d" % b)
+        count("CN", 144 * b, view("CM", o, o + 288))
+    act(view("TG"), view("R1"), AF.Sign, bias=view("TS", 64, 65), scale=-1.0)
+    if r > 0:
+        act(waste(view("TG", 0, 32 * r)), view("TG", 0, 32 * r), AF.Relu, acc=view("TA", 0, 1))
+        named("TA.0")
+    else:
+        fill(view("TA", 0, 1), 0.0)
+    if r < N - 1:
+        act(waste(view("TG", 32 * r, 224)), view("TG", 32 * r, 224), AF.Relu, scale=-1.0, acc=view("TA", 1, 2))
+        named("TA.1")
+    else:
+        fill(view("TA", 1, 2), 0.0)
+    ts(view("CN", 431, 432), view("CN", 319, 320), view("TA", 0, 1), SUB, view("TA", 1, 2), ADD)
+    for a in (0, 1):
+        copy(quarter("CA", a, 0, 3), quarter("CN", 1 - a, 143, 432, 144))
+        copy(quarter("CA", a, 3, 6), quarter("CN", 2, 143, 432, 144))
+    for b in range(3):
+        spread(half("E0", 0, 32 * b, 32 * b + 32), half("CN", 0, 144 * b + 143, 144 * b + 144))
+        ts(half("EX3", 0, 32 * b, 32 * b + 32), half("E0", 0, 32 * b, 32 * b + 32), half("CA", 0, b, b + 1), ADD,
+           half("CA", 0, 3 + b, 4 + b), ADD)
+    turn(half("PR", 0), half("EX3", 0))
+    turn(half("PR", 1), half("EX3", 0))
+    ts(view("OH"), view("PR"), view("JC"), EQ)
+    tt(view("M2"), view("OH"), view("KV"), MUL)
+    sums(view("XS", 1, 2), view("M2"))
+    tt(view("M1"), view("OH"), view("VR"), MUL)
+    sums(view("XS", 0, 1), view("M1"))
+    to_all(view("XS"), "X2L", 4, 2, "x2")
+    arrive("x2", 7 * lanes, [view("X2L", 4, 18)])
+
+    fill(view("X2L", 2, 4), 0.0)
+    copy(view("X2L", 0, 2), view("XS"))
+    for i in range(8):
+        mm((1 + i) % 8, "QA" if i < 4 else "QB", 128 * (i % 4), "SRC", H0 + P, P + HN)
+    quant("SRC", AA * P, 2 * P, "GO")
+    quant("SRC", BA * P, 2 * P, "GO", 768)
+    for h in range(2):
+        ts(view("PC", h, h + 1), view("PB"), 16.0 * h, ADD, E - 1.0, MIN)
+    swap("WC", 4, True)
+    act(view("P2"), view("PC"), bias=2.0 * E * r, scale=2.0)
+    act(view("PN"), view("PC"), bias=2.0 * E * r + 2.0, scale=2.0)
+    act(view("NN"), view("PC", 1, 2), bias=-2.0 * E * r - 2.0, scale=-2.0)
+    act(view("NS"), view("PC"), bias=-2.0 * E * r - 1.0, scale=-2.0)
+    act(view("W", 256, 528, step=264), view("PC"), bias=2.0 * E * r - 128.0 - 2.0 * P * r, scale=2.0)
+    act(view("W", 260, 528, step=264), view("PC"), bias=2.0 * E * r - 128.0 - 2.0 * P * (r + 1), scale=2.0)
+    act(view("H2"), view("PF"), bias=2.0 * E * r, scale=2.0)
+    act(view("NH"), view("PF"), bias=-2.0 * E * r - 1.0, scale=-2.0)
+    act(view("WH", 128, 129), view("PF"), bias=4.0 * E * r - 256.0, scale=4.0)
+    if r == 0:
+        fill(view("W", 258, 528, step=264), 0.0)
+    if r == N - 1:
+        fill(view("W", 259, 528, step=264), 0.0)
+    quant("QW", 0, 128, "WT")
+    for i in range(8):
+        e0 = 672 * (i // 4)
+        copy(view("HG", e0 + i % 4, e0 + 672, step=4), bank((1 + i) % 8, P + HN), 0.0625)
+    quant("SRC", H0 + AA * P, P + HN, "HG")
+    quant("SRC", H0 + BA * P, P + HN, "HG", 672)
+
+    sc, mc = view("EX2", 0, 1), view("EX2", 64, 65)
+    for k, row in ((0, "DS"), (1, "DN")):
+        sums(view("SC", k, k + 1), view("X2L", k, 18, step=2))
+        spread(view("EX2", 64 * k, 64 * k + 32), view("SC", k, k + 1))
+        for h in (0, 1):
+            spread(half("EX2", h, 64 * k + 32, 64 * k + 64), half("SC", 1 - h, k, k + 1))
+        turn(view(row, 0, 64), view("EX2", 64 * k, 64 * k + 64))
+        swap(row, 32)
+    act(view("SG"), view("DS"), AF.Sign, bias=sc, scale=-1.0)
+    ts(view("LO"), view("DN"), mc, GE, -0.5, MUL)
+    tt(view("BF"), view("SG"), view("LO"), LE)
+    count("P1", 0, view("BF"))
+    ts(view("EXM"), view("THR"), view("P1", 63, 64), ADD, mc, MAX)
+    turn(view("MR", 0, 32), view("EXM"))
+    for h in (0, 1):
+        turn(half("MR", h, 32, 64), half("EXM", 1 - h))
+    swap("MR", 32)
+    signs(view("MR"), view("EXM", 0, 1), view("RK"), -1.0)
+    ts(view("F0"), view("EXM", 0, 1), 0.5 / UNIT, MUL, view("FC"), ADD)
+    spread(view("F32"), view("F0"))
+    if r > 0:
+        signs(view("MR"), (4.0 * P * r - 0.5) * UNIT, view("SB", 0, 1), -1.0)
+    if r < N - 1:
+        signs(view("MR"), (4.0 * P * (r + 1) - 0.5) * UNIT, view("SB", 1, 2), -1.0)
+    spread(view("EXF", 0, 32), view("RK"), view("F32"))
+    for h in (0, 1):
+        spread(half("EXF", h, 32, 64), half("RK", 1 - h), half("F32", 1 - h))
+    turn(view("FR", 0, 64), view("EXF"))
+    swap("FR", 32)
+
+    for h in range(2):
+        signs(view("FR"), view("NS", h, h + 1), view("W", 264 * h + 257, 264 * h + 258))
+    act(view("AB"), view("FR"), AF.Abs, bias=view("NN"))
+    for k in range(4):
+        c = 264 + 128 + 32 * k
+        act(view("W", c, c + 32), view("AB", 32 * k, 32 * k + 32), AF.Relu, bias=view("WC", 4 * k + 1, 4 * k + 2), scale=view("WC", 4 * k + 3, 4 * k + 4))
+    if r > 0:
+        ts(view("W", 258, 528, step=264), view("W", 256, 528, step=264), view("SB", 0, 1), LT, 2.0 * (H0 + 64 - 8 * r), MUL)
+        named("low")
+    if r < N - 1:
+        ts(view("W", 259, 528, step=264), view("W", 260, 528, step=264), view("SB", 1, 2), GE, 2.0 * (H0 - 32 - 8 * r), MUL)
+        named("high")
+    for h in range(2):
+        for k in range(4):
+            f, c = view("FR", 32 * k, 32 * k + 32), 264 * h + 32 * k
+            ts(view("W", c, c + 32), f, view("P2", h, h + 1), EQ, view("WC", 4 * k, 4 * k + 1), MUL)
+            if h == 0:
+                ts(view("W", c + 128, c + 160), f, view("PN", h, h + 1), EQ, view("WC", 4 * k + 1, 4 * k + 2), MUL)
+    for h in range(2):
+        count("OF", 130 * h, view("W", 264 * h, 264 * h + 260))
+    for a in range(4):
+        for b in range(4):
+            copy(quarter("OTF", b, 2 * a, 2 * a + 2), quarter("OF", a, 129, 260, 130))
+    ts(view("OT"), view("OTF"), 0.5, MUL)
+    op("v", lambda e, q: e.tensor_copy(T.RUN[:, 0:128].bitcast(dt.uint32), T.SRC[:, 0:ALL].bitcast(dt.uint32).indirect(T.OT[:, 0:8])),
+       [view("SRC"), view("OT")], [view("RUN")], 0.26)
+    op("s", lambda e, q: e.activation(T.sRUN[:, 0:128], T.sSRC[:, 0:ALL].indirect(T.OT[:, 0:8]), AF.Copy),
+       [view("sSRC"), view("OT")], [view("sRUN")], 0.28)
+
+    mm(0, "QW", 0, "RUN", 0, 128)
+    copy(view("YT"), bank(0, E))
+    store(lambda e: e.dma_start(T.y[:, 0:E], T.YT[:]), view("YT"), "o5")
+    store(lambda e: e.dma_start(T.oc[:, 0:4 * E], T.RUN[:, 0:E].bitcast(dt.uint8)), view("RUN", 0, E), "o0")
+    for k in range(4):
+        store(lambda e, k=k: e.dma_start(T.osc[4 * k:4 * k + 4, 0:E], T.sRUN[32 * k:32 * k + 4, 0:E]), view("sRUN", 0, E, 32 * k, 32 * k + 4), "o%d" % (1 + k))
+    for k in (129, 130):
+        signs(view("FR"), view("NH"), view("WH", k, k + 1))
+    for k in range(4):
+        ts(view("WH", 32 * k, 32 * k + 32), view("FR", 32 * k, 32 * k + 32), view("H2"), EQ, view("WC", 4 * k + 2, 4 * k + 3), MUL)
+    sums(view("HB"), view("WH", 0, 131))
+    store(lambda e: e.dma_start(T.hs[0:1, 0:E], T.HB[0:E, 0:1]), view("HB", 0, 1, 0, E), "o6")
+
+    order, queue = place(ops, *links(ops), ORDER)
+    total = {}
+    known = {k: {} for k in queues}
+    clocks = {}
+    log = {}
+
+    def await_(q, need):
+        for s, n in sorted(need.items()):
+            if known[q].get(s, 0) < n:
+                queues[q].wait_ge(T.sem[s], n)
+                for s2, n2 in clocks.get((s, n), {}).items():
+                    known[q][s2] = max(known[q].get(s2, 0), n2)
+                known[q][s] = n
+
+    for i in order:
+        o, q = ops[i], queue[i]
+        sem = o["sem"] or q
+        if o["fn"] is not None:
+            need = {}
+            for w, wr in accesses(o):
+                for v, vr, s, n, q2 in log.get(w[0], []):
+                    if (wr or vr or (w[0] == "ps" and q2 != q)) and meet(wide(w), v):
+                        need[s] = max(need.get(s, 0), n)
+            await_(q, need)
+            ins = o["fn"](queues[q], q)
+            if o["local"]:
+                ins.then_inc(T.sem[sem], o["inc"])
+            total[sem] = total.get(sem, 0) + o["inc"]
+            clocks[(sem, total[sem])] = dict(known[q])
+        else:
+            total[sem] = o["inc"]
+        for w, wr in accesses(o):
+            w = wide(w)
+            l = log.setdefault(w[0], [])
+            if wr:
+                l[:] = [e for e in l if not holds(w, e[0])]
+            l.append((w, wr, sem, total[sem], q))
+    await_("y", total)

@@ -7,38 +7,37 @@ AA, AB, BA, BB = 6, 7, 11, 12
 H0 = 3 * P
 HN = 72
 ALL = H0 + BB * P + HN
+MA, MB = 2049.0, 2048.0
 UNIT = 2.0 ** -20
 HUGE = 1.0e29
 CODE = "float8_e4m3fn_x4"
 HALF = "bfloat16"
-CYCLE, SYNC, OWN, FLY, LOCAL = 0.0009, 0.16, 0.14, 1.6, 2.0
+CYCLE, FLY, LOCAL = 0.0009, 1.6, 2.0
 ORDER = """
-load.u:s XT.0.384:v load.x:y Z32.0.0:v U0.0.8:v load.a:y KAP.3.0:s PI.0.0:q PM.0.1:v KAP.0.0:s VR.3.0:v THR.2.0:s ZB.0.0:v
-PF.0.0:v PM.0.0:v X16.0.0:v WC.1.2:s load.b:s X32.0.0:v PA.0.0:v QV.0.0:v load.w:y KAP.1.0:s WC.1.0:s SRC.0.0:v WC.1.1:s
-HK.0.288:v FI.0.0:q UT.0.3:v UT.0.1:v WC.2.3:s WC.3.2:s JC.0.0:s ps.0.0:p X1S.0.0:s KAP.2.0:s UT.0.0:v UT.0.2:v XA.0.0:v
-WC.0.0:s XB.0.0:v QU.0.0:v XB.0.2:v PB.0.0:v H2.0.0:s X2L.0.2:v ps.0.512:p XB.0.1:v SROW.0.0:s KV.0.0:v send.x1:q PC.0.0:v
-FC.1.0:s WC.1.3:s WC.2.2:s SQ.0.0:s PC.0.1:v WC.3.1:s TS.0.0:v THR.0.0:s WH.0.128:s WC.3.3:s JC.2.0:v codes.1:q WC.0.2:s
-SQ.2.0:s scales.1:q TRI.0.32:v QA.0.0:v QB.0.0:v WC.0.1:s SQ.3.0:v WC.3.0:s SQ.1.0:s ps.0.1024:p WC.2.1:s KT.0.2:s ps.0.1536:p
-OE.0.32:v OE.0.64:v ps.0.0.2:p VR.2.0:s ps.0.3584:p ps.0.3072:p FC.2.0:s KT.0.3:s WC.0.3:s TRI.0.64:v FC.3.0:s CM.0.512:v
-W.0.256:s codes.0:q OE.0.0:v CM.0.544:v TRI.0.0:v KT.0.0:v come.x1:- WC.2.4:s KT.0.387:s CM.0.800:v CM.0.224:v ps.0.2560:p
-CM.0.832:v CM.0.256:v EX1.0.192:v NS.0.0:s EX1.0.64:s ps.0.2048:p EX1.0.32:v EX1.0.96:s KT.0.386:s P2.0.0:s EX1.0.160:v
-ps.0.512.2:p FC.0.0:s KT.0.385:s EX1.0.0:v KT.0.384:s EX1.0.128:v KT.0.1:s R1.0.0:v WC.2.8:s CN.0.288:v GE.0:v GE.1:v
-scales.0:q SRC.0.96:v TG.0.0:s TA.1:s TA.0:s GT.0:v W.0.260:s WC.2.0:s GT.1:v NH.0.0:s CN.0.0:v WC.0.4:s CN.0.144:v E0.0.0:s
-CN.0.431:v CA.0.0:v CA.1.3:v CA.0.3:v ps.0.0.3:p CA.1.0:v E0.0.32:s PN.0.0:s WC.3.8:s THR.1.0:s E0.0.64:v VR.0.0:s EX3.0.0:v
-VR.1.0:s EX3.0.64:v EX3.0.32:v PR.2.0:v PR.0.0:v OH.0.0:v come.halo:- THR.3.0:s M2.0.0:v M1.0.0:v ps.0.2048.2:p ps.0.512.3:p
-XS.0.0:v ps.0.1536.2:p XS.0.1:s HK.0.2:v ps.0.3584.2:p WC.0.8:v HK.0.0:s X2L.0.0:s HK.0.386:s HK.0.3:v ps.0.1024.2:p
-ps.0.3072.2:p ps.0.2560.2:p GO.0.2:s WC.1.8:s NN.0.0:s ps.0.0.4:p send.x2:q HK.0.1:v GO.0.0:s HK.0.385:s GO.0.1:v GO.0.3:s
-QW.0.0:v HK.0.384:s GO.0.769:s GO.0.770:v SRC.0.576:v come.x2:- HK.0.387:v SRC.0.384:v SC.0.0:s SC.0.1:s GO.0.771:v EX2.0.32:v
-EX2.2.32:s EX2.0.0:s EX2.2.96:s EX2.0.96:v EX2.0.64:s DS.0.0:v GO.0.768:s ps.0.1536.3:p DS.1.64:s ps.0.3072.3:p DS.3.64:s
-DN.0.0:v ps.0.2048.3:p DS.0.64:v DN.0.64:s ps.0.1024.3:p DN.3.64:s DS.2.64:v SG.0.0:s DN.1.64:v DN.2.64:v SRC.0.1056:v LO.0.0:v
-ps.0.512.4:p HG.0.2:s HG.0.3:s HG.0.1:s BF.0.0:v P1.0.0:v HG.0.673:s HG.0.0:s EXM.0.0:v MR.0.0:v ps.0.2560.3:p MR.2.32:v
-HG.0.672:s MR.0.32:v F0.0.0:v MR.3.64:v MR.1.64:v F32.0.0:v MR.2.64:s ps.0.3584.3:p MR.0.64:s ps.0.0.5:p HG.0.674:s sg.RK.0:s
-EXF.2.32:s EXF.0.32:s SRC.0.864:v HG.0.675:v EXF.0.0:s SRC.0.1344:v FR.0.0:v FR.2.64:v FR.0.64:v sg.SB.1:s sg.SB.0:s FR.3.64:s
-FR.1.64:s W.0.32:v high:v low:v W.0.0:v W.0.264:v AB.0.0:s W.0.360:v sg.W.257:s W.0.392:s W.0.192:v W.0.96:v W.0.160:v
-W.0.224:v W.0.64:v W.0.128:v W.0.328:v sg.W.521:s W.0.488:s W.0.424:s W.0.296:v OF.0.0:v W.0.456:s OF.0.130:v WH.0.0:v
-OTF.2.6:v OTF.0.0:s OTF.2.0:v OTF.2.4:s OTF.0.2:v OTF.0.6:s OTF.1.4:v OTF.1.6:s OTF.2.2:s OTF.3.0:s OTF.0.4:v OTF.1.2:v
-OTF.3.4:v OTF.1.0:s OTF.3.2:v OTF.3.6:v OT.0.0:v sg.WH.129:s sRUN.0.0:s sg.WH.130:s RUN.0.0:v WH.0.64:v WH.0.96:v WH.0.32:v
-store.o2:y ps.0.0.6:p store.o4:s store.o3:y store.o1:y HB.0.0:s YT.0.0:s store.o5:s store.o0:y store.o6:y
+load.u:s KK.0.0:v KK.0.32:v XT.0.384:v load.x:y Z32.0.0:v FC.0.1:s FC.1.1:s U0.0.8:v load.a:y PI.0.0:q PM.0.1:v
+ZB.0.0:v load.b:s FC.2.1:s FC.3.1:s PF.0.0:v PM.0.0:v KAP.0.0:s WC.3.1:s X16.0.0:v X32.0.0:v PA.0.0:v PB.0.0:v HK.0.288:v KAP.2.0:s
+PC.0.0:v SRC.0.0:v QV.0.0:v WC.0.0:s UT.0.3:v load.w:y FC.3.0:s UT.0.0:v ps.0.0:p X1S.0.0:s KAP.1.0:s WC.2.1:s FI.0.0:q UT.0.2:v
+UT.0.1:v PC.0.1:v XA.0.0:v X2L.0.18:v WC.3.0:s LH.0.2:s QU.0.0:v first:q XB.0.1:v send.x1:q KAP.3.0:s ps.0.512:p I0.0.0:s LH.0.0:s
+SROW.0.0:s XB.0.2:v VR.3.0:v PN.0.0:s WC.1.1:s codes.1:q SQ.2.0:s SQ.0.0:s TRI.0.64:v WC.0.1:s XB.0.0:v TRI.0.0:v TRI.0.32:v
+codes.0:q KV.0.0:v TS.0.0:v SQ.3.0:v QA.0.0:v P2.0.0:s QB.0.0:v ps.0.0.2:p ps.0.1536:p SQ.1.0:s FC.2.0:s OE.0.32:v ps.0.1024:p
+OE.0.0:v CM.0.512:v OE.0.64:v WC.1.0:s KT.0.0:s CM.0.256:v CM.0.800:v CM.0.832:v come.x1:- LH.0.4:s EX1.0.0:v KT.0.3:s EX1.0.128:v
+EX1.0.32:v EX1.0.192:v ps.0.2048:p FC.0.0:s KT.0.2:s JC.0.0:s scales.0:q ps.0.3584:p WC.2.0:s EX1.0.64:s CM.0.544:v EX1.0.160:s
+EX1.0.96:s KT.0.387:s ps.0.3072:p CN.0.288:v R1.0.0:v ps.0.2560:p come.halo:- CM.0.224:v GT.1:v KT.0.386:s KT.0.384:s GE.1:v
+GT.0:v GE.0:v KT.0.385:s TG.0.0:s ps.0.512.2:p CN.0.144:v KT.0.1:s TA.1:s SRC.0.96:v TA.0:s VR.2.0:s CN.0.0:v CN.0.431:v
+ps.0.0.3:p E0.0.32:s E0.0.0:v ps.0.1024.2:p ps.0.1536.2:p CA.1.0:s CA.0.3:v CA.0.0:v CA.1.3:s E0.0.64:v VR.0.0:s VR.1.0:s WC.0.2:s
+EX3.0.32:v EX3.0.0:v EX3.0.64:v JC.2.0:v PR.0.0:v ps.0.3584.2:p ps.0.2048.2:p PR.2.0:v OH.0.0:v WC.1.4:v M2.0.0:v XS.0.1:s
+HK.0.2:s ps.0.512.3:p ps.0.3072.2:p M1.0.0:v XS.0.0:v HK.0.1:v LH.0.6:s ps.0.0.4:p QW.0.0:v ps.0.2560.2:p send.x2:q FC.1.0:s
+X2L.0.16:v HK.0.0:v GO.0.1:v HK.0.3:s GO.0.0:s HK.0.385:v GO.0.3:s WC.0.4:v WC.2.2:s GO.0.2:v SRC.0.576:v HK.0.386:s WC.3.4:s
+HK.0.387:s come.x2:- GO.0.769:v HK.0.384:s SRC.0.384:v EX2.0.81:v GO.0.771:s EX2.0.1:v DN.2.32:v GO.0.768:s ps.0.2048.3:p
+GO.0.770:s DS.0.0:v ps.0.512.4:p ps.0.2560.3:p ps.0.1536.3:p DS.0.32:v DN.0.0:v DN.0.32:v DS.2.64:v DS.2.32:v DS.0.64:s
+ps.0.3072.3:p DN.0.64:v DS.1.32:s SRC.0.1056:v DN.2.64:s DN.1.32:s LO.0.0:v SG.0.0:s ps.0.1024.3:p HG.0.3:s EXM.3.0:v NH.0.0:s
+HG.0.672:s HG.0.0:s BF.0.0:v WC.2.4:v P1.0.0:v HG.0.2:s HG.0.1:s H2.0.0:s EXM.0.0:v MR.2.32:v MR.0.0:v MR.0.32:v MR.3.64:v
+MR.1.64:v MR.2.64:s ps.0.0.5:p MR.0.64:s F0.0.1:v sg.RK.0:s F0.0.0:v sg.SB.0:s H4.0.0:v EXF.0.64:s ps.0.3584.3:p SRC.0.864:v
+EXF.0.32:s EXF.0.0:s EXF.2.96:v EXF.0.96:v EXF.2.32:v FB.0.0:v FR.0.0:v WH.0.128:s FB.0.64:v FB.1.64:v FR.0.64:v sg.SB.1:s
+FB.2.64:s FB.3.64:s high:v low:v W.0.396:v W.0.132:v FR.2.64:s FR.1.64:s FR.3.64:s W.0.0:v W.0.264:v OF.0.0:v HG.0.675:s
+HG.0.673:s HG.0.674:s OF.0.130:v OTF.1.0:s SRC.0.1344:v OTF.0.0:v OTF.0.2:v OTF.1.2:s OTF.3.4:s OTF.3.6:v OTF.2.6:v OT.2.0:v
+OTF.2.4:s OT.0.0:v sg.WH.129:s OT.0.4:v OT.2.4:v sRUN.0.0:s sg.WH.130:s WH.0.32:v store.o2:y RUN.0.0:v ps.0.0.6:p YT.0.0:s
+store.o3:y store.o1:s WH.0.64:v store.o0:y store.o5:s WH.0.0:v WH.0.96:v HB.0.0:v store.o4:y store.o6:y
 """
 
 
@@ -57,16 +56,16 @@ SCRATCH = {
     "RUN": _sb(128, CODE), "sRUN": _sb(128, "uint8"), "YT": _sb(E),
     "ps": ("psum", [128, 4096], "float32"),
     "Z32": _sb(32), "PI": _sb(1, "int32"), "PM": _sb(2, "int32"), "PF": _sb(1), "X32": _sb(1), "X16": _sb(1),
-    "FI": _sb(96), "XA": _sb(1), "XB": _sb(3), "TRI": _sb(96), "JC": _sb(1), "KAP": _sb(1), "KV": _sb(96), "VR": _sb(96), "FC": _sb(1),
-    "PA": _sb(1), "PB": _sb(1), "PC": _sb(2), "P2": _sb(2), "PN": _sb(2), "NN": _sb(1), "NS": _sb(2), "H2": _sb(1), "NH": _sb(1),
-    "WC": _sb(16), "THR": _sb(32),
+    "FI": _sb(96), "XA": _sb(1), "XB": _sb(3), "TRI": _sb(96), "JC": _sb(1), "KAP": _sb(1), "KV": _sb(96), "VR": _sb(96), "FC": _sb(2),
+    "PA": _sb(1), "PB": _sb(1), "PC": _sb(2), "P2": _sb(2), "PN": _sb(2), "H2": _sb(1), "NH": _sb(1),
+    "WC": _sb(8), "KK": _sb(64), "LH": _sb(8), "I0": _sb(2), "H4": _sb(4),
     "X1S": _sb(1), "X1L": _sb(7), "SROW": _sb(96), "SQ": _sb(32), "TS": _sb(96), "OE": _sb(96),
     "EX1": _sb(224), "R1": _sb(224), "CM": _sb(864, HALF), "CN": _sb(432, HALF), "CA": _sb(6), "TG": _sb(224, HALF), "TA": _sb(2),
     "E0": _sb(96), "EX3": _sb(96), "PR": _sb(96), "OH": _sb(96), "M1": _sb(96), "M2": _sb(96),
-    "XS": _sb(2), "X2L": _sb(20), "SC": _sb(2), "EX2": _sb(128), "DS": _sb(128), "DN": _sb(128), "SG": _sb(128, HALF), "LO": _sb(128, HALF),
-    "BF": _sb(128, HALF), "P1": _sb(64), "EXM": _sb(32), "MR": _sb(128),
-    "F0": _sb(1), "F32": _sb(32), "RK": _sb(1), "SB": _sb(2), "EXF": _sb(64), "FR": _sb(128), "J4": _sb(2304),
-    "W": _sb(528), "AB": _sb(128), "OF": _sb(260), "OTF": _sb(8), "OT": _sb(8, "uint16"),
+    "XS": _sb(2), "X2L": _sb(84), "EX2": _sb(160), "DS": _sb(96), "DN": _sb(96), "SG": _sb(96, HALF), "LO": _sb(96, HALF),
+    "BF": _sb(96, HALF), "P1": _sb(48), "EXM": _sb(32), "MR": _sb(128),
+    "F0": _sb(2), "RK": _sb(1), "SB": _sb(2), "EXF": _sb(128), "FR": _sb(128), "FB": _sb(128), "J4": _sb(2304),
+    "W": _sb(528), "OF": _sb(260), "OTF": _sb(8), "OT": _sb(8, "uint16"),
     "WH": _sb(132), "HB": _sb(1),
 }
 COUNTERS = ["v", "s", "p", "q"]
@@ -118,7 +117,7 @@ def accesses(o):
 
 
 def links(ops):
-    n, log = len(ops), {}
+    log = {}
     before = [dict() for _ in ops]
     last = None
     for i, o in enumerate(ops):
@@ -156,54 +155,22 @@ def place(ops, before, keys, table):
     missing = [len(b) for b in before]
     ready = [i for i in range(n) if missing[i] == 0]
     queue = [""] * n
-    if table:
-        rank = {}
-        for k, x in enumerate(table.split()):
-            x = x.split(":")
-            rank[x[0]] = (float(k), x[1])
-        at, order = [0.0] * n, []
-        for i in range(n):
-            at[i], queue[i] = rank.get(keys[i], (max([at[j] for j in before[i]], default=0.0) + 0.5, ops[i]["qs"][:1] or "-"))
-        while ready:
-            i = min(ready, key=lambda k: (at[k], k))
-            ready.remove(i)
-            order.append(i)
-            for k in after[i]:
-                missing[k] -= 1
-                if missing[k] == 0:
-                    ready.append(k)
-        return order, queue
-    way = [0.0] * n
-    for i in reversed(range(n)):
-        o = ops[i]
-        way[i] = o["cost"] + o["lag"] + max([way[k] + before[k][i] + OWN for k in after[i]], default=0.0)
-    busy = {}
-    start, end = [0.0] * n, [0.0] * n
+    rank = {}
+    for k, x in enumerate(table.split()):
+        x = x.split(":")
+        rank[x[0]] = (float(k), x[1])
+    at, order = [0.0] * n, []
+    for i in range(n):
+        at[i], queue[i] = rank.get(keys[i], (max([at[j] for j in before[i]], default=0.0) + 0.5, ops[i]["qs"][:1] or "-"))
     while ready:
-        i = max(ready, key=lambda k: (way[k], -k))
+        i = min(ready, key=lambda k: (at[k], k))
         ready.remove(i)
-        o, best = ops[i], None
-        for q in o["qs"] or ["-"]:
-            t = 0.0
-            for j, gap in before[i].items():
-                wake = 0.0 if q == "-" else SYNC if queue[j] != q else OWN if q in "vs" else 0.0
-                t = max(t, end[j] + gap + wake)
-            if q != "-":
-                for s, e in busy.setdefault(q, []):
-                    if t + o["cost"] <= s + 1e-9:
-                        break
-                    t = max(t, e)
-            if best is None or t < best[0] - 1e-9:
-                best = (t, q)
-        start[i], queue[i] = best
-        end[i] = start[i] + o["cost"] + o["lag"]
-        if queue[i] != "-":
-            busy[queue[i]] = sorted(busy[queue[i]] + [(start[i], start[i] + o["cost"])])
+        order.append(i)
         for k in after[i]:
             missing[k] -= 1
             if missing[k] == 0:
                 ready.append(k)
-    return sorted(range(n), key=lambda i: (start[i], i)), queue
+    return order, queue
 
 
 def rank_program(g, core, T, topo):
@@ -253,14 +220,21 @@ def rank_program(g, core, T, topo):
             return e.activation(ap(o), ap(i), AF.Copy) if scale is None else e.activation(ap(o), ap(i), AF.Copy, scale=scale)
         op(qs, fn, [i], [o], time(width(i)))
 
-    def spread(o, x, z=None):
-        z = z or view("Z32", 0, 32, x[1], x[2])
+    def spread(o, x):
+        z = view("Z32", 0, 32, x[1], x[2])
 
         def fn(e, q):
             if q == "v":
                 return e.tensor_scalar(ap(o), ap(z), ap(x), None, ADD)
             return e.activation(ap(o), ap(z), AF.Identity, bias=ap(x))
         op("vs", fn, [z, x], [o], time(32))
+
+    def lay(o, z, x, y):
+        def fn(e, q):
+            if q == "v":
+                return e.tensor_scalar(ap(o), ap(z), ap(x), ap(y), MUL, ADD)
+            return e.activation(ap(o), ap(z), AF.Identity, bias=ap(y), scale=ap(x))
+        op("vs", fn, [z, x, y], [o], time(32))
 
     junk = [0]
 
@@ -277,11 +251,14 @@ def rank_program(g, core, T, topo):
             return e.activation(ap(j), ap(i), AF.Copy, accum_out=ap(o))
         op("vs", fn, [i], [o, j], time(width(i)) + 0.01)
 
+    def scan(o, x, y, first=0.0, op1=ADD):
+        op("v", lambda e, q: e.tensor_tensor_scan(ap(o), ap(x), ap(y), val(first), ADD, op1),
+           [x, y] + ([first] if isinstance(first, tuple) else []), [o], time(width(x), o, x))
+
     def count(name, c0, i, first=0.0):
         n, p0, p1, a, b, _ = i
         m = (a + b) // 2
-        o, x, y = view(name, c0, c0 + m - a, p0, p1), view(n, a, m, p0, p1), view(n, m, b, p0, p1)
-        op("v", lambda e, q: e.tensor_tensor_scan(ap(o), ap(x), ap(y), first, ADD, ADD), [x, y], [o], time(m - a, o, x))
+        scan(view(name, c0, c0 + m - a, p0, p1), view(n, a, m, p0, p1), view(n, m, b, p0, p1), first)
 
     def signs(i, bias, acc, scale=1.0):
         act(waste(i), i, AF.Sign, bias=bias, scale=scale, acc=acc)
@@ -348,16 +325,18 @@ def rank_program(g, core, T, topo):
         op("q", lambda e, q: e.remote_dma_fused([tr], local_sem=T.sem.left), [src], [], 1.0, "left", lanes, False, FLY)
         named("send." + sem)
 
-    def to_one(d, d0, s0, n):
+    def to_one(d, d0, s0, n, parts, key=None):
         rid, pid = topo.addr(T.cores[d], core)
         m = topo.mask(core, T.cores[d])
         ln = bin(m).count("1")
         c, s = view("SRC", s0, s0 + n), view("sSRC", s0, s0 + n)
         oc, os = T.SRC[:, d0:d0 + n].bitcast(dt.uint8), T.sSRC[:, d0:d0 + n]
-        op("q", lambda e, q: e.remote_dma(oc, ap(c).bitcast(dt.uint8), T.sem.halo, T.sem.left, pid, rid, m), [c], [], 0.7, "left", ln, False, FLY)
-        named("codes.%d" % (d > r))
-        op("q", lambda e, q: e.remote_dma(os, ap(s), T.sem.halo, T.sem.left, pid, rid, m), [s], [], 0.7, "left", ln, False, FLY)
-        named("scales.%d" % (d > r))
+        if "c" in parts:
+            op("q", lambda e, q: e.remote_dma(oc, ap(c).bitcast(dt.uint8), T.sem.halo, T.sem.left, pid, rid, m), [c], [], 0.7, "left", ln, False, FLY)
+            named("codes.%d" % (d > r))
+        if "s" in parts:
+            op("q", lambda e, q: e.remote_dma(os, ap(s), T.sem.halo, T.sem.left, pid, rid, m), [s], [], 0.7, "left", ln, False, FLY)
+            named(key or "scales.%d" % (d > r))
 
     def arrive(sem, n, writes):
         ops.append({"qs": "", "fn": None, "rd": [], "wr": writes, "cost": 0.0, "sem": sem, "inc": n, "local": False, "lag": 0.0,
@@ -384,10 +363,9 @@ def rank_program(g, core, T, topo):
     tt(view("PB"), view("PA"), view("X16"), ADD)
     alpha, beta, sigma = (BA - 1, BB, 2, 2), (AA, AB - 2, 1, 1), (1, 3, 1, 2)
     for a in range(4):
-        for buf, c, v in (("KAP", 0, (4.0 * P * r + sigma[a]) * UNIT), ("FC", 0, 2.0 - 0.5 * sigma[a] + 127.0), ("WC", 0, 2.0 * P * alpha[a]),
-                          ("WC", 1, 2.0 * P * beta[a]), ("WC", 2, float(sigma[a])), ("WC", 3, -2.0 * P * beta[a])):
+        for buf, c, v in (("KAP", 0, (4.0 * P * r + sigma[a]) * UNIT), ("FC", 0, MA * (129.0 - 0.5 * sigma[a]) + 2.0 * P * alpha[a]),
+                          ("FC", 1, MB * (129.0 - 0.5 * sigma[a]) - 2.0 * P * beta[a]), ("WC", 0, 2.0 * P * alpha[a]), ("WC", 1, float(sigma[a]))):
             act(quarter(buf, a, c, c + 1), quarter("Z32", a, 0, 1), bias=v)
-        act(quarter("THR", a), quarter("Z32", a), bias=0.5 - K if a < 3 else -1000.0)
     quant("QV", 0, 128, "U0")
     quant("SRC", 0, 128, "XT")
 
@@ -398,12 +376,14 @@ def rank_program(g, core, T, topo):
     quant("QU", 0, 128, "UT")
     mm(1, "QU", 0, "SRC", 0, 128)
     copy(view("SROW"), bank(1, 96))
+    up, down = (r + 1, H0, P - (56 - 8 * r), 56 - 8 * r), (r - 1, H0 + HN - 8 * r, 0, 8 * r)
+    to_one(*(up if r < N - 1 else down), "s", "first")
     to_all(view("X1S"), "X1L", 0, 1, "x1")
     arrive("x1", 7 * lanes, [view("X1L")])
     if r < N - 1:
-        to_one(r + 1, H0, P - (56 - 8 * r), 56 - 8 * r)
+        to_one(*up, "c")
     if r > 0:
-        to_one(r - 1, H0 + HN - 8 * r, 0, 8 * r)
+        to_one(*down, "cs" if r < N - 1 else "c")
     land, cnt = [], 0
     if r > 0:
         land += [view("SRC", H0, H0 + 64 - 8 * r), view("sSRC", H0, H0 + 64 - 8 * r)]
@@ -498,31 +478,34 @@ def rank_program(g, core, T, topo):
     sums(view("XS", 1, 2), view("M2"))
     tt(view("M1"), view("OH"), view("VR"), MUL)
     sums(view("XS", 0, 1), view("M1"))
-    to_all(view("XS"), "X2L", 4, 2, "x2")
-    arrive("x2", 7 * lanes, [view("X2L", 4, 18)])
+    to_all(view("XS"), "X2L", 2, 2, "x2")
+    arrive("x2", 7 * lanes, [view("X2L", 2, 16)])
 
-    fill(view("X2L", 2, 4), 0.0)
-    copy(view("X2L", 0, 2), view("XS"))
+    fill(view("X2L", 18, 84), 0.0)
+    copy(view("X2L", 16, 18), view("XS"))
     for i in range(8):
         mm((1 + i) % 8, "QA" if i < 4 else "QB", 128 * (i % 4), "SRC", H0 + P, P + HN)
     quant("SRC", AA * P, 2 * P, "GO")
     quant("SRC", BA * P, 2 * P, "GO", 768)
     for h in range(2):
         ts(view("PC", h, h + 1), view("PB"), 16.0 * h, ADD, E - 1.0, MIN)
-    swap("WC", 4, True)
-    act(view("P2"), view("PC"), bias=2.0 * E * r, scale=2.0)
-    act(view("PN"), view("PC"), bias=2.0 * E * r + 2.0, scale=2.0)
-    act(view("NN"), view("PC", 1, 2), bias=-2.0 * E * r - 2.0, scale=-2.0)
-    act(view("NS"), view("PC"), bias=-2.0 * E * r - 1.0, scale=-2.0)
-    act(view("W", 256, 528, step=264), view("PC"), bias=2.0 * E * r - 128.0 - 2.0 * P * r, scale=2.0)
-    act(view("W", 260, 528, step=264), view("PC"), bias=2.0 * E * r - 128.0 - 2.0 * P * (r + 1), scale=2.0)
-    act(view("H2"), view("PF"), bias=2.0 * E * r, scale=2.0)
-    act(view("NH"), view("PF"), bias=-2.0 * E * r - 1.0, scale=-2.0)
+    swap("WC", 2, True)
+    fill(view("KK", 0, 32), MA)
+    fill(view("KK", 32, 64), MB)
+    for k, m in ((0, MA), (1, MB)):
+        for j in (0, 1):
+            act(view("LH", 4 * k + 2 * j, 4 * k + 2 * j + 2), view("PC"), bias=2.0 * m * (E * r + j), scale=2.0 * m)
+    act(view("I0"), view("PC"), bias=-254.0 * E * r - 256.0 - 2.0 * P * r, scale=-254.0)
+    act(view("P2"), view("PC"), bias=2.0 * E * r - 128.0 - 2.0 * P * r, scale=2.0)
+    act(view("PN"), view("PC"), bias=2.0 * E * r - 128.0 - 2.0 * P * (r + 1), scale=2.0)
+    act(view("H2"), view("PF"), bias=2.0 * MA * E * r, scale=2.0 * MA)
+    ts(view("H4"), view("WC", 0, 8, step=2), view("H2"), ADD)
+    act(view("NH"), view("PF"), bias=-2.0 * MA * (E * r + 1), scale=-2.0 * MA)
     act(view("WH", 128, 129), view("PF"), bias=4.0 * E * r - 256.0, scale=4.0)
     if r == 0:
-        fill(view("W", 258, 528, step=264), 0.0)
+        fill(view("W", 128, 528, step=264), 0.0)
     if r == N - 1:
-        fill(view("W", 259, 528, step=264), 0.0)
+        fill(view("W", 260, 528, step=264), 0.0)
     quant("QW", 0, 128, "WT")
     for i in range(8):
         e0 = 672 * (i // 4)
@@ -530,60 +513,57 @@ def rank_program(g, core, T, topo):
     quant("SRC", H0 + AA * P, P + HN, "HG")
     quant("SRC", H0 + BA * P, P + HN, "HG", 672)
 
-    sc, mc = view("EX2", 0, 1), view("EX2", 64, 65)
+    sc, mc = view("EX2", 8, 9, 0, 96), view("EX2", 88, 89, 0, 96)
     for k, row in ((0, "DS"), (1, "DN")):
-        sums(view("SC", k, k + 1), view("X2L", k, 18, step=2))
-        spread(view("EX2", 64 * k, 64 * k + 32), view("SC", k, k + 1))
-        for h in (0, 1):
-            spread(half("EX2", h, 64 * k + 32, 64 * k + 64), half("SC", 1 - h, k, k + 1))
-        turn(view(row, 0, 64), view("EX2", 64 * k, 64 * k + 64))
-        swap(row, 32)
-    act(view("SG"), view("DS"), AF.Sign, bias=sc, scale=-1.0)
-    ts(view("LO"), view("DN"), mc, GE, -0.5, MUL)
-    tt(view("BF"), view("SG"), view("LO"), LE)
-    count("P1", 0, view("BF"))
-    ts(view("EXM"), view("THR"), view("P1", 63, 64), ADD, mc, MAX)
+        c = 80 * k + 8
+        scan(view("EX2", c - 7, c + 32), view("X2L", 2 + k, 80 + k, step=2), view("X2L", 18, 57))
+        turn(view(row, 0, 32, 0, 96), view("EX2", c, c + 32, 0, 96))
+        for a in (0, 2):
+            turn(quarter(row, a, 32, 64), quarter("EX2", 2 - a, c, c + 32))
+            copy(quarter(row, a, 64, 96), quarter(row, 1, 0, 32))
+        copy(quarter(row, 1, 32, 96), quarter(row, 0, 0, 64))
+    ds, dn, sg, lo, bf = [view(x, 0, 96, 0, 96) for x in ("DS", "DN", "SG", "LO", "BF")]
+    act(sg, ds, AF.Sign, bias=sc, scale=-1.0)
+    ts(lo, dn, mc, GE, -0.5, MUL)
+    tt(bf, sg, lo, LE)
+    count("P1", 0, bf, 0.5 - K)
+    ts(view("EXM", 0, 32, 0, 96), view("Z32", 0, 32, 0, 96), view("P1", 47, 48, 0, 96), ADD, mc, MAX)
+    copy(quarter("EXM", 3), quarter("EX2", 3, 88, 120))
     turn(view("MR", 0, 32), view("EXM"))
     for h in (0, 1):
         turn(half("MR", h, 32, 64), half("EXM", 1 - h))
     swap("MR", 32)
     signs(view("MR"), view("EXM", 0, 1), view("RK"), -1.0)
-    ts(view("F0"), view("EXM", 0, 1), 0.5 / UNIT, MUL, view("FC"), ADD)
-    spread(view("F32"), view("F0"))
+    for k, m in ((0, MA), (1, MB)):
+        ts(view("F0", k, k + 1), view("EXM", 0, 1), 0.5 / UNIT * m, MUL, view("FC", k, k + 1), ADD)
     if r > 0:
         signs(view("MR"), (4.0 * P * r - 0.5) * UNIT, view("SB", 0, 1), -1.0)
     if r < N - 1:
         signs(view("MR"), (4.0 * P * (r + 1) - 0.5) * UNIT, view("SB", 1, 2), -1.0)
-    spread(view("EXF", 0, 32), view("RK"), view("F32"))
-    for h in (0, 1):
-        spread(half("EXF", h, 32, 64), half("RK", 1 - h), half("F32", 1 - h))
-    turn(view("FR", 0, 64), view("EXF"))
-    swap("FR", 32)
+    for k, row in ((0, "FR"), (1, "FB")):
+        lay(view("EXF", 64 * k, 64 * k + 32), view("KK", 32 * k, 32 * k + 32), view("RK"), view("F0", k, k + 1))
+        for h in (0, 1):
+            lay(half("EXF", h, 64 * k + 32, 64 * k + 64), half("KK", 1 - h, 32 * k, 32 * k + 32), half("RK", 1 - h), half("F0", 1 - h, k, k + 1))
+        turn(view(row, 0, 64), view("EXF", 64 * k, 64 * k + 64))
+        swap(row, 32)
 
-    for h in range(2):
-        signs(view("FR"), view("NS", h, h + 1), view("W", 264 * h + 257, 264 * h + 258))
-    act(view("AB"), view("FR"), AF.Abs, bias=view("NN"))
-    for k in range(4):
-        c = 264 + 128 + 32 * k
-        act(view("W", c, c + 32), view("AB", 32 * k, 32 * k + 32), AF.Relu, bias=view("WC", 4 * k + 1, 4 * k + 2), scale=view("WC", 4 * k + 3, 4 * k + 4))
     if r > 0:
-        ts(view("W", 258, 528, step=264), view("W", 256, 528, step=264), view("SB", 0, 1), LT, 2.0 * (H0 + 64 - 8 * r), MUL)
+        ts(view("W", 128, 528, step=264), view("P2"), view("SB", 0, 1), LT, 2.0 * (H0 + 64 - 8 * r), MUL)
         named("low")
     if r < N - 1:
-        ts(view("W", 259, 528, step=264), view("W", 260, 528, step=264), view("SB", 1, 2), GE, 2.0 * (H0 - 32 - 8 * r), MUL)
+        ts(view("W", 260, 528, step=264), view("PN"), view("SB", 1, 2), GE, -2.0 * (H0 - 32 - 8 * r), MUL)
         named("high")
     for h in range(2):
-        for k in range(4):
-            f, c = view("FR", 32 * k, 32 * k + 32), 264 * h + 32 * k
-            ts(view("W", c, c + 32), f, view("P2", h, h + 1), EQ, view("WC", 4 * k, 4 * k + 1), MUL)
-            if h == 0:
-                ts(view("W", c + 128, c + 160), f, view("PN", h, h + 1), EQ, view("WC", 4 * k + 1, 4 * k + 2), MUL)
-    for h in range(2):
-        count("OF", 130 * h, view("W", 264 * h, 264 * h + 260))
+        for k, row in ((0, "FR"), (1, "FB")):
+            c = 264 * h + 132 * k
+            ts(view("W", c, c + 128), view(row), view("LH", 4 * k + h, 4 * k + h + 1), MAX, view("LH", 4 * k + 2 + h, 4 * k + 3 + h), MIN)
+        scan(view("OF", 130 * h, 130 * h + 129), view("W", 264 * h, 264 * h + 129), view("W", 264 * h + 132, 264 * h + 261), view("I0", h, h + 1), SUB)
     for a in range(4):
-        for b in range(4):
-            copy(quarter("OTF", b, 2 * a, 2 * a + 2), quarter("OF", a, 129, 260, 130))
-    ts(view("OT"), view("OTF"), 0.5, MUL)
+        for b in (a, a ^ 1):
+            copy(quarter("OTF", b, 2 * a, 2 * a + 2), quarter("OF", a, 128, 260, 130))
+    for d in (0, 1):
+        for h in (0, 1):
+            ts(half("OT", d, 4 * h, 4 * h + 4), half("OTF", h, 4 * h, 4 * h + 4), 0.5, MUL)
     op("v", lambda e, q: e.tensor_copy(T.RUN[:, 0:128].bitcast(dt.uint32), T.SRC[:, 0:ALL].bitcast(dt.uint32).indirect(T.OT[:, 0:8])),
        [view("SRC"), view("OT")], [view("RUN")], 0.26)
     op("s", lambda e, q: e.activation(T.sRUN[:, 0:128], T.sSRC[:, 0:ALL].indirect(T.OT[:, 0:8]), AF.Copy),
@@ -598,7 +578,7 @@ def rank_program(g, core, T, topo):
     for k in (129, 130):
         signs(view("FR"), view("NH"), view("WH", k, k + 1))
     for k in range(4):
-        ts(view("WH", 32 * k, 32 * k + 32), view("FR", 32 * k, 32 * k + 32), view("H2"), EQ, view("WC", 4 * k + 2, 4 * k + 3), MUL)
+        ts(view("WH", 32 * k, 32 * k + 32), view("FR", 32 * k, 32 * k + 32), view("H4", k, k + 1), EQ, view("WC", 2 * k + 1, 2 * k + 2), MUL)
     sums(view("HB"), view("WH", 0, 131))
     store(lambda e: e.dma_start(T.hs[0:1, 0:E], T.HB[0:E, 0:1]), view("HB", 0, 1, 0, E), "o6")
 

@@ -8,36 +8,37 @@ H0 = 3 * P
 HN = 72
 ALL = H0 + BB * P + HN
 MA, MB = 2049.0, 2048.0
+SEQ = "C01 C12 C23 C34 C45 C56 C67 C70 Y01 q1 q2 q4 H02 H13 H24 H35 Y16 Y27 H40 H51 H62 H73 q3 q5 Y44 Y35 Y56"
+TOP = 2.0 ** 31
 UNIT = 2.0 ** -20
 HUGE = 1.0e29
 CODE = "float8_e4m3fn_x4"
 HALF = "bfloat16"
-CYCLE, FLY, LOCAL = 0.0009, 1.6, 2.0
 ORDER = """
-load.u:s KK.0.0:v KK.0.32:v XT.0.384:v load.x:y Z32.0.0:v FC.0.1:s FC.1.1:s U0.0.8:v load.a:y PI.0.0:q PM.0.1:v
-ZB.0.0:v load.b:s FC.2.1:s FC.3.1:s PF.0.0:v PM.0.0:v KAP.0.0:s WC.3.1:s X16.0.0:v X32.0.0:v PA.0.0:v PB.0.0:v HK.0.288:v KAP.2.0:s
-PC.0.0:v SRC.0.0:v QV.0.0:v WC.0.0:s UT.0.3:v load.w:y FC.3.0:s UT.0.0:v ps.0.0:p X1S.0.0:s KAP.1.0:s WC.2.1:s FI.0.0:q UT.0.2:v
-UT.0.1:v PC.0.1:v XA.0.0:v X2L.0.18:v WC.3.0:s LH.0.2:s QU.0.0:v first:q XB.0.1:v send.x1:q KAP.3.0:s ps.0.512:p I0.0.0:s LH.0.0:s
-SROW.0.0:s XB.0.2:v VR.3.0:v PN.0.0:s WC.1.1:s codes.1:q SQ.2.0:s SQ.0.0:s TRI.0.64:v WC.0.1:s XB.0.0:v TRI.0.0:v TRI.0.32:v
-codes.0:q KV.0.0:v TS.0.0:v SQ.3.0:v QA.0.0:v P2.0.0:s QB.0.0:v ps.0.0.2:p ps.0.1536:p SQ.1.0:s FC.2.0:s OE.0.32:v ps.0.1024:p
-OE.0.0:v CM.0.512:v OE.0.64:v WC.1.0:s KT.0.0:s CM.0.256:v CM.0.800:v CM.0.832:v come.x1:- LH.0.4:s EX1.0.0:v KT.0.3:s EX1.0.128:v
-EX1.0.32:v EX1.0.192:v ps.0.2048:p FC.0.0:s KT.0.2:s JC.0.0:s scales.0:q ps.0.3584:p WC.2.0:s EX1.0.64:s CM.0.544:v EX1.0.160:s
-EX1.0.96:s KT.0.387:s ps.0.3072:p CN.0.288:v R1.0.0:v ps.0.2560:p come.halo:- CM.0.224:v GT.1:v KT.0.386:s KT.0.384:s GE.1:v
-GT.0:v GE.0:v KT.0.385:s TG.0.0:s ps.0.512.2:p CN.0.144:v KT.0.1:s TA.1:s SRC.0.96:v TA.0:s VR.2.0:s CN.0.0:v CN.0.431:v
-ps.0.0.3:p E0.0.32:s E0.0.0:v ps.0.1024.2:p ps.0.1536.2:p CA.1.0:s CA.0.3:v CA.0.0:v CA.1.3:s E0.0.64:v VR.0.0:s VR.1.0:s WC.0.2:s
-EX3.0.32:v EX3.0.0:v EX3.0.64:v JC.2.0:v PR.0.0:v ps.0.3584.2:p ps.0.2048.2:p PR.2.0:v OH.0.0:v WC.1.4:v M2.0.0:v XS.0.1:s
-HK.0.2:s ps.0.512.3:p ps.0.3072.2:p M1.0.0:v XS.0.0:v HK.0.1:v LH.0.6:s ps.0.0.4:p QW.0.0:v ps.0.2560.2:p send.x2:q FC.1.0:s
-X2L.0.16:v HK.0.0:v GO.0.1:v HK.0.3:s GO.0.0:s HK.0.385:v GO.0.3:s WC.0.4:v WC.2.2:s GO.0.2:v SRC.0.576:v HK.0.386:s WC.3.4:s
-HK.0.387:s come.x2:- GO.0.769:v HK.0.384:s SRC.0.384:v EX2.0.81:v GO.0.771:s EX2.0.1:v DN.2.32:v GO.0.768:s ps.0.2048.3:p
-GO.0.770:s DS.0.0:v ps.0.512.4:p ps.0.2560.3:p ps.0.1536.3:p DS.0.32:v DN.0.0:v DN.0.32:v DS.2.64:v DS.2.32:v DS.0.64:s
-ps.0.3072.3:p DN.0.64:v DS.1.32:s SRC.0.1056:v DN.2.64:s DN.1.32:s LO.0.0:v SG.0.0:s ps.0.1024.3:p HG.0.3:s EXM.3.0:v NH.0.0:s
-HG.0.672:s HG.0.0:s BF.0.0:v WC.2.4:v P1.0.0:v HG.0.2:s HG.0.1:s H2.0.0:s EXM.0.0:v MR.2.32:v MR.0.0:v MR.0.32:v MR.3.64:v
-MR.1.64:v MR.2.64:s ps.0.0.5:p MR.0.64:s F0.0.1:v sg.RK.0:s F0.0.0:v sg.SB.0:s H4.0.0:v EXF.0.64:s ps.0.3584.3:p SRC.0.864:v
-EXF.0.32:s EXF.0.0:s EXF.2.96:v EXF.0.96:v EXF.2.32:v FB.0.0:v FR.0.0:v WH.0.128:s FB.0.64:v FB.1.64:v FR.0.64:v sg.SB.1:s
-FB.2.64:s FB.3.64:s high:v low:v W.0.396:v W.0.132:v FR.2.64:s FR.1.64:s FR.3.64:s W.0.0:v W.0.264:v OF.0.0:v HG.0.675:s
-HG.0.673:s HG.0.674:s OF.0.130:v OTF.1.0:s SRC.0.1344:v OTF.0.0:v OTF.0.2:v OTF.1.2:s OTF.3.4:s OTF.3.6:v OTF.2.6:v OT.2.0:v
-OTF.2.4:s OT.0.0:v sg.WH.129:s OT.0.4:v OT.2.4:v sRUN.0.0:s sg.WH.130:s WH.0.32:v store.o2:y RUN.0.0:v ps.0.0.6:p YT.0.0:s
-store.o3:y store.o1:s WH.0.64:v store.o0:y store.o5:s WH.0.0:v WH.0.96:v HB.0.0:v store.o4:y store.o6:y
+U0.0.8:v load.x:y MK.0.0:v load.u:s PI.0.0:q W.0.128:v Z32.0.0:v WC.2.0:s WC.3.1:s PM.0.0:v TA.0.0:v WC.2.1:s PF.0.0:v FC.1.1:s XT.0.384:v
+WC.1.0:s ZB.0.0:v X1L.0.260:v X32.0.0:v XS.3.0:v X1L.0.4:v WC.1.1:s MK.0.0.2:v HK.0.288:v PA.0.0:v SRC.0.0:v UT.0.2:v WC.0.0:s UT.0.0:v
+WC.0.1:s FC.3.0:s UT.0.3:v KAP.0.0:s UT.0.1:v KAP.2.0:s WC.3.0:s QV.0.0:v FI.0.0:q load.a:y WC.2.2:s XA.0.0:v X1L.0.132:v H2.0.0:s NH.0.0:s
+QU.0.0:v ps.0.0:p X1L.0.388:v PM.0.1:v FC.1.0:s JR.0.0:v ps.0.512:p FC.2.0:s WC.0.2:s load.b:y FC.0.1:s XB.0.0:v WC.2.4:s FC.3.1:s FC.0.0:s
+first:q KAP.1.0:s WC.1.4:s WC.0.4:s XB.0.1:v KAP.3.0:s XB.0.2:v WC.3.4:s X1S.0.0:s FC.2.1:s WH.0.128:s SROW.0.0:s QA.0.0:v SQ.3.0:s TRI.0.64:v
+SQ.0.0:s send.x1:q ps.0.512.2:p SQ.2.0:s codes.1:q SQ.1.0:s TS.0.0:v ps.0.1024:p ps.0.0.2:p QB.0.0:v OE.0.64:v OE.0.32:v OE.0.0:v TRI.0.0:v
+VR.1.0:s codes.0:q TRI.0.32:v KT.0.1:s CM.0.512:v KT.0.2:s KT.0.0:s CM.0.832:v ps.0.1536:p CM.0.800:v CM.0.224:v X16.0.0:v SRC.0.224:v
+KT.0.3:s ps.0.3072:p ps.0.3584:p KT.0.386:s come.x1:- CM.0.544:v KT.0.387:s ps.0.2048:p ps.0.2560:p KT.0.384:s CN.0.288:v KT.0.385:s
+EX1.0.192:s top.0:v EX1.0.128:s EX1.0.0:v CM.0.256:v EX1.0.64:v EX1.0.160:s TG.0.224:v R1.0.0:v scales.0:q top.384:v R1.0.64:v R1.0.128:v
+TG.0.0:s SRC.0.96:v TG.0.128:s JR.0.32:v GE.0:v TA.0:s GT.0:v GE.1:v come.halo:- ps.0.0.3:p TA.1:s GT.1:v CN.0.0:v VR.0.0:s mC0:p CN.0.144:v
+CA.1.5:s CA.1.2:v E0.0.64:v CA.0.2:s mC1:p E0.0.0:v CA.0.3:v CA.1.3:v CA.0.5:s X2L.0.18:v CA.0.0:s CA.1.0:s E0.0.32:s mC4:p PB.0.0:v mC2:p
+EX3.0.64:v HK.0.0:s EX3.0.0:v EX3.0.32:v VR.2.0:s KV.0.0:v HK.0.1:s mC3:p GO.0.0:s mC5:p HK.0.384:s OH.2.0:v load.w:y OH.0.0:v PC.0.0:v
+GO.0.1:s PC.0.1:v M1.0.0:v M1.0.96:v mC6:p XS.0.0:v GO.0.768:s XS.0.1:v send.x2:q HK.0.2:s NL.0.0:s mC7:p BF.0.96:v PN.0.0:s YS.0.360:v
+LH.0.2:s H4.0.0:v LH.0.0:s YS.0.552:v HK.0.3:s KK.0.0:v GO.0.2:s come.x2:- HK.0.385:v QW.0.0:v X2L.0.16:s GO.0.3:s HK.0.386:s YS.0.1032:v
+GO.0.769:s YS.0.768:v HK.0.387:s W.0.397:v KK.0.32:v GO.0.770:s hop.0:v SRC.0.576:v hop.384:v mY0:p LH.0.6:s YS.0.1248:v GO.0.771:s YS.0.0:s
+W.0.396:s YS.0.192:s mY2:p SRC.0.384:v P2.0.0:s mH1:p mH0:p mH3:p I0.0.0:s YS.0.576:s SRC.0.1056:v EX2.0.1:v EX2.0.137:v mH2:p DS.0.0:v
+DS.2.64:s mH5:p DS.0.32:v DN.0.0:v DS.1.32:s DN.0.32:v DS.2.32:v DN.0.64:s DS.0.64:v DN.2.32:v DN.2.64:s DN.1.32:v SG.0.0:s mH4:p HG.0.1:v
+HG.0.0:s LO.0.0:v HG.0.3:s mH6:p EX2.0.41:v HG.0.2:s BF.0.0:v EXM.3.103:v EXM.0.0:v SRC.0.864:v MR.2.32:v MR.0.0:v MR.0.32:v mH7:p LH.0.4:s
+HG.0.673:s HG.0.672:s HG.0.674:s MR.3.64:v MR.1.64:v HG.0.675:v F0.0.1:v MR.2.64:s MR.0.64:s sg.RK.0:s mY1:p F0.0.0:v YS.0.384:s EXF.0.64:s
+EXF.0.0:s SRC.0.1344:v EXF.2.32:s EXF.2.96:v sg.SB.0:s EXF.0.96:v EXF.0.32:v mY4:p FB.0.0:v mY3:p sg.SB.1:s FR.0.0:v FB.2.64:s FB.3.64:s
+FR.3.64:s FB.0.64:v FR.2.64:s FB.1.64:v FR.1.64:v low:v WH.0.0:v high:v W.0.132:v FR.0.64:s mY5:p TW.0.0:s I1:s W.0.0:v YS.0.1344:s W.0.264:v
+OF.0.0:v OF.0.130:v WH.0.96:v WH.0.64:v WH.0.32:v YS.0.1056:s OTF.1.2:s OTF.0.0:s OTF.0.2:v OTF.2.4:s OTF.1.0:v OTF.3.4:v OTF.3.6:s
+sg.WH.129:s OTF.2.6:v OT.0.0:v OT.2.0:v OT.0.4:v sg.WH.130:s OT.2.4:v YS.0.864:s HB.0.0:s YT.0.0:s RUN.0.0:v sRUN.0.0:v store.o6:y store.o0:y
+store.o5:s store.o1:y store.o2:s store.o4:y store.o3:y
 """
 
 
@@ -45,41 +46,25 @@ def _sb(n, d="float32"):
     return ("sbuf", [128, n], d)
 
 
-SCRATCH = {
-    "XT": _sb(512, HALF), "U0": _sb(512, HALF), "UT": _sb(512, HALF), "ZB": _sb(128, HALF),
-    "AT": _sb(2048, HALF), "BT": _sb(2048, HALF), "WT": _sb(512, HALF),
-    "QU": _sb(128, CODE), "sQU": _sb(128, "uint8"), "QV": _sb(128, CODE), "sQV": _sb(128, "uint8"),
-    "QA": _sb(512, CODE), "sQA": _sb(512, "uint8"), "QB": _sb(512, CODE), "sQB": _sb(512, "uint8"),
-    "QW": _sb(128, CODE), "sQW": _sb(128, "uint8"),
-    "SRC": _sb(ALL, CODE), "sSRC": _sb(ALL, "uint8"),
-    "KT": _sb(768, HALF), "GO": _sb(1536, HALF), "HK": _sb(672, HALF), "HG": _sb(1344, HALF),
-    "RUN": _sb(128, CODE), "sRUN": _sb(128, "uint8"), "YT": _sb(E),
-    "ps": ("psum", [128, 4096], "float32"),
-    "Z32": _sb(32), "PI": _sb(1, "int32"), "PM": _sb(2, "int32"), "PF": _sb(1), "X32": _sb(1), "X16": _sb(1),
-    "FI": _sb(96), "XA": _sb(1), "XB": _sb(3), "TRI": _sb(96), "JC": _sb(1), "KAP": _sb(1), "KV": _sb(96), "VR": _sb(96), "FC": _sb(2),
-    "PA": _sb(1), "PB": _sb(1), "PC": _sb(2), "P2": _sb(2), "PN": _sb(2), "H2": _sb(1), "NH": _sb(1),
-    "WC": _sb(8), "KK": _sb(64), "LH": _sb(8), "I0": _sb(2), "H4": _sb(4),
-    "X1S": _sb(1), "X1L": _sb(7), "SROW": _sb(96), "SQ": _sb(32), "TS": _sb(96), "OE": _sb(96),
-    "EX1": _sb(224), "R1": _sb(224), "CM": _sb(864, HALF), "CN": _sb(432, HALF), "CA": _sb(6), "TG": _sb(224, HALF), "TA": _sb(2),
-    "E0": _sb(96), "EX3": _sb(96), "PR": _sb(96), "OH": _sb(96), "M1": _sb(96), "M2": _sb(96),
-    "XS": _sb(2), "X2L": _sb(84), "EX2": _sb(160), "DS": _sb(96), "DN": _sb(96), "SG": _sb(96, HALF), "LO": _sb(96, HALF),
-    "BF": _sb(96, HALF), "P1": _sb(48), "EXM": _sb(32), "MR": _sb(128),
-    "F0": _sb(2), "RK": _sb(1), "SB": _sb(2), "EXF": _sb(128), "FR": _sb(128), "FB": _sb(128), "J4": _sb(2304),
-    "W": _sb(528), "OF": _sb(260), "OTF": _sb(8), "OT": _sb(8, "uint16"),
-    "WH": _sb(132), "HB": _sb(1),
-}
-COUNTERS = ["v", "s", "p", "q"]
-DMAS = ["dx", "du", "da", "db", "dw", "w2", "w3", "o0", "o1", "o2", "o3", "o4", "o5", "o6"]
-SEMAPHORES = COUNTERS + DMAS + ["x1", "x2", "halo", "left"]
+SCRATCH = {"ps": ("psum", [128, 4096], "float32")}
+for _d, _l in ((HALF, "XT:512 U0:512 UT:512 ZB:128 AT:2048 BT:2048 WT:512 KT:768 GO:1536 HK:672 HG:1344 CM:864 CN:432 TG:226 SG:96 LO:96"),
+               (CODE, "QU:128 QV:128 QA:512 QB:512 QW:128 SRC:%d RUN:128" % ALL), ("int32", "PI:1 PM:2"), ("uint16", "OT:8"),
+               ("float32", "YT:128 YS:1512 Z32:32 PF:1 X32:1 X16:1 FI:96 JR:64 E0:96 XA:1 XB:3 TRI:96 KAP:1 KV:96 VR:96 FC:2 PA:1 PB:1 PC:2 P2:2 PN:2 "
+                "H2:1 NH:1 WC:8 KK:64 LH:8 I0:2 H4:4 X1S:1 X1L:516 SROW:96 SQ:32 TS:96 OE:96 EX1:224 R1:224 CA:6 TA:2 MK:64 NL:1 TW:128 EX3:96 "
+                "OH:96 M1:192 XS:2 X2L:84 EX2:176 BF:135 DS:96 DN:96 EXM:135 MR:128 F0:2 RK:1 SB:2 EXF:128 FR:128 FB:128 J4:2560 W:528 OF:260 "
+                "OTF:8 WH:132 HB:1")):
+    for _x in _l.split():
+        SCRATCH[_x.split(":")[0]] = _sb(int(_x.split(":")[1]), _d)
+        if _d == CODE:
+            SCRATCH["s" + _x.split(":")[0]] = _sb(int(_x.split(":")[1]), "uint8")
+SEMAPHORES = "v s p q dx du da db dw o0 o1 o2 o3 o4 o5 o6 x1 x2 halo left".split()
 AF = ActivationFunctionType
 ADD, SUB, MUL, MIN, MAX = AluOpType.add, AluOpType.subtract, AluOpType.mult, AluOpType.min, AluOpType.max
 GT, GE, LT, LE, EQ = AluOpType.is_gt, AluOpType.is_ge, AluOpType.is_lt, AluOpType.is_le, AluOpType.is_equal
 
 
 def view(name, c0=0, c1=None, p0=0, p1=128, step=1):
-    if c1 is None:
-        c1 = SCRATCH[name][1][1]
-    return (name, p0, p1, c0, c1, step)
+    return (name, p0, p1, c0, SCRATCH[name][1][1] if c1 is None else c1, step)
 
 
 def quarter(name, a, c0=0, c1=None, step=1):
@@ -97,9 +82,7 @@ def width(w):
 def meet(a, b):
     if a[1] >= b[2] or b[1] >= a[2] or a[3] >= b[4] or b[3] >= a[4]:
         return False
-    if a[5] == 1 and b[5] == 1:
-        return True
-    return bool(set(range(a[3], a[4], a[5])) & set(range(b[3], b[4], b[5])))
+    return (a[5] == 1 and b[5] == 1) or bool(set(range(a[3], a[4], a[5])) & set(range(b[3], b[4], b[5])))
 
 
 def holds(a, b):
@@ -107,9 +90,7 @@ def holds(a, b):
 
 
 def wide(w):
-    if w[0] != "ps":
-        return w
-    return ("ps", 0, 128, w[3] // 512 * 512, (w[4] + 511) // 512 * 512, 1)
+    return w if w[0] != "ps" else ("ps", 0, 128, w[3] // 512 * 512, (w[4] + 511) // 512 * 512, 1)
 
 
 def accesses(o):
@@ -117,19 +98,17 @@ def accesses(o):
 
 
 def links(ops):
-    log = {}
-    before = [dict() for _ in ops]
-    last = None
+    log, before, last = {}, [set() for _ in ops], None
     for i, o in enumerate(ops):
         for w, wr in accesses(o):
             for v, vr, j in log.get(w[0], []):
                 if j != i and (wr or vr or w[0] == "ps") and meet(wide(w), v):
-                    before[i].setdefault(j, 0.0)
+                    before[i].add(j)
         if "behind" in o:
-            before[i][o["behind"]] = 0.0
+            before[i].add(o["behind"])
         if o["qs"] == "q":
             if last is not None:
-                before[i].setdefault(last, -ops[last]["lag"])
+                before[i].add(last)
             last = i
         for w, wr in accesses(o):
             w = wide(w)
@@ -154,14 +133,15 @@ def place(ops, before, keys, table):
             after[j].append(i)
     missing = [len(b) for b in before]
     ready = [i for i in range(n) if missing[i] == 0]
-    queue = [""] * n
-    rank = {}
+    queue, rank = [""] * n, {}
     for k, x in enumerate(table.split()):
         x = x.split(":")
         rank[x[0]] = (float(k), x[1])
     at, order = [0.0] * n, []
     for i in range(n):
-        at[i], queue[i] = rank.get(keys[i], (max([at[j] for j in before[i]], default=0.0) + 0.5, ops[i]["qs"][:1] or "-"))
+        at[i], queue[i] = rank.get(keys[i], (max([at[j] for j in before[i]], default=0.0) + 0.5, "-"))
+        if queue[i] not in ops[i]["qs"]:
+            queue[i] = ops[i]["qs"][:1] or "-"
     while ready:
         i = min(ready, key=lambda k: (at[k], k))
         ready.remove(i)
@@ -184,57 +164,34 @@ def rank_program(g, core, T, topo):
         n, p0, p1, c0, c1, st = w
         return T[n][p0:p1, c0:c1] if st == 1 else T[n][p0:p1, c0:c1:st]
 
-    def op(qs, fn, reads, writes, cost, sem=None, inc=1, local=True, lag=0.0):
-        ops.append({"qs": qs, "fn": fn, "rd": reads, "wr": writes, "cost": cost, "sem": sem, "inc": inc, "local": local, "lag": lag})
-
-    def named(key):
-        ops[-1]["key"] = key
+    def op(qs, fn, reads, writes, key=None, sem=None, inc=1, local=True):
+        ops.append({"qs": qs, "fn": fn, "rd": [x for x in reads if isinstance(x, tuple)], "wr": writes, "sem": sem, "inc": inc, "local": local, "key": key})
 
     def val(x):
         return ap(x) if isinstance(x, tuple) else x
 
-    def time(n, *sides):
-        if sides and all(SCRATCH[w[0]][2] == HALF for w in sides):
-            n = n / 2
-        return max(64, n) * CYCLE
+    def act(o, i, func=AF.Copy, bias=None, scale=None, acc=None, key=None):
+        kw = {k: val(x) for k, x in (("bias", bias), ("scale", scale), ("accum_out", acc)) if x is not None}
+        op("s", lambda e, q: e.activation(ap(o), ap(i), func, **kw), [i, bias, scale], [o] + ([acc] if acc else []), key)
 
-    def act(o, i, func=AF.Copy, bias=None, scale=None, acc=None):
-        kw = {}
-        for k, x in (("bias", bias), ("scale", scale), ("accum_out", acc)):
-            if x is not None:
-                kw[k] = val(x)
-        op("s", lambda e, q: e.activation(ap(o), ap(i), func, **kw), [i] + [x for x in (bias, scale) if isinstance(x, tuple)],
-           [o] + ([acc] if acc is not None else []), time(width(i)) + (0.025 if acc is not None else 0.0))
-
-    def ts(o, i, s1, op0, s2=None, op1=None):
-        rd = [i] + [s for s in (s1, s2) if isinstance(s, tuple)]
-        if op1 is None:
-            op("v", lambda e, q: e.tensor_scalar(ap(o), ap(i), val(s1), None, op0), rd, [o], time(width(i), o, i))
-        else:
-            op("v", lambda e, q: e.tensor_scalar(ap(o), ap(i), val(s1), val(s2), op0, op1), rd, [o], time(width(i), o, i))
+    def ts(o, i, s1, op0, s2=None, op1=None, key=None):
+        op("v", lambda e, q: e.tensor_scalar(ap(o), ap(i), val(s1), val(s2), *([op0] if op1 is None else [op0, op1])), [i, s1, s2], [o], key)
 
     def copy(o, i, scale=None, qs="vs"):
         def fn(e, q):
             if q == "v":
                 return e.tensor_copy(ap(o), ap(i)) if scale is None else e.tensor_scalar(ap(o), ap(i), scale, None, MUL)
             return e.activation(ap(o), ap(i), AF.Copy) if scale is None else e.activation(ap(o), ap(i), AF.Copy, scale=scale)
-        op(qs, fn, [i], [o], time(width(i)))
+        op(qs, fn, [i], [o])
 
-    def spread(o, x):
-        z = view("Z32", 0, 32, x[1], x[2])
-
-        def fn(e, q):
-            if q == "v":
-                return e.tensor_scalar(ap(o), ap(z), ap(x), None, ADD)
-            return e.activation(ap(o), ap(z), AF.Identity, bias=ap(x))
-        op("vs", fn, [z, x], [o], time(32))
+    def spread(o, x, z=None):
+        z = z or view("Z32", 0, 32, x[1], x[2])
+        op("vs", lambda e, q: e.tensor_scalar(ap(o), ap(z), ap(x), None, ADD) if q == "v" else e.activation(ap(o), ap(z), AF.Identity, bias=ap(x)),
+           [z, x], [o])
 
     def lay(o, z, x, y):
-        def fn(e, q):
-            if q == "v":
-                return e.tensor_scalar(ap(o), ap(z), ap(x), ap(y), MUL, ADD)
-            return e.activation(ap(o), ap(z), AF.Identity, bias=ap(y), scale=ap(x))
-        op("vs", fn, [z, x, y], [o], time(32))
+        op("vs", lambda e, q: e.tensor_scalar(ap(o), ap(z), ap(x), ap(y), MUL, ADD) if q == "v"
+           else e.activation(ap(o), ap(z), AF.Identity, bias=ap(y), scale=ap(x)), [z, x, y], [o])
 
     junk = [0]
 
@@ -244,16 +201,11 @@ def rank_program(g, core, T, topo):
 
     def sums(o, i):
         j = waste(i)
+        op("vs", lambda e, q: e.tensor_reduce(ap(o), ap(i), AxisListType.X, ADD) if q == "v"
+           else e.activation(ap(j), ap(i), AF.Copy, accum_out=ap(o)), [i], [o, j])
 
-        def fn(e, q):
-            if q == "v":
-                return e.tensor_reduce(ap(o), ap(i), AxisListType.X, ADD)
-            return e.activation(ap(j), ap(i), AF.Copy, accum_out=ap(o))
-        op("vs", fn, [i], [o, j], time(width(i)) + 0.01)
-
-    def scan(o, x, y, first=0.0, op1=ADD):
-        op("v", lambda e, q: e.tensor_tensor_scan(ap(o), ap(x), ap(y), val(first), ADD, op1),
-           [x, y] + ([first] if isinstance(first, tuple) else []), [o], time(width(x), o, x))
+    def scan(o, x, y, first=0.0, op1=ADD, op0=ADD):
+        op("v", lambda e, q: e.tensor_tensor_scan(ap(o), ap(x), ap(y), val(first), op0, op1), [x, y, first], [o])
 
     def count(name, c0, i, first=0.0):
         n, p0, p1, a, b, _ = i
@@ -261,17 +213,16 @@ def rank_program(g, core, T, topo):
         scan(view(name, c0, c0 + m - a, p0, p1), view(n, a, m, p0, p1), view(n, m, b, p0, p1), first)
 
     def signs(i, bias, acc, scale=1.0):
-        act(waste(i), i, AF.Sign, bias=bias, scale=scale, acc=acc)
-        named("sg.%s.%d" % (acc[0], acc[3]))
+        act(waste(i), i, AF.Sign, bias, scale, acc, "sg.%s.%d" % (acc[0], acc[3]))
 
     def tt(o, a, b, o0):
-        op("v", lambda e, q: e.tensor_tensor(ap(o), ap(a), ap(b), o0), [a, b], [o], time(2 * width(a)))
+        op("v", lambda e, q: e.tensor_tensor(ap(o), ap(a), ap(b), o0), [a, b], [o])
 
     def fill(o, c):
-        op("v", lambda e, q: e.memset(ap(o), c), [], [o], time(width(o), o))
+        op("v", lambda e, q: e.memset(ap(o), c), [], [o])
 
     def turn(o, i):
-        op("v", lambda e, q: e.transpose(ap(o), ap(i)), [i], [o], time(width(i)))
+        op("v", lambda e, q: e.transpose(ap(o), ap(i)), [i], [o])
 
     def swap(name, n, both=False):
         if both:
@@ -282,48 +233,34 @@ def rank_program(g, core, T, topo):
 
     def quant(dst, c0, n, src, e0=0):
         o, s, i = view(dst, c0, c0 + n), view("s" + dst, c0, c0 + n), view(src, e0, e0 + 4 * n)
-        op("v", lambda e, q: e.quantize_mx(ap(o), ap(s), ap(i)), [i], [o, s], 0.015 + 0.001 * n)
+        op("v", lambda e, q: e.quantize_mx(ap(o), ap(s), ap(i)), [i], [o, s])
 
-    def mm(bk, w, wc, x, xc, n):
+    def mm(bk, w, wc, x, xc, n, key=None):
         o = view("ps", 512 * bk, 512 * bk + n)
         a, sa, b, sb = view(w, wc, wc + 128), view("s" + w, wc, wc + 128), view(x, xc, xc + n), view("s" + x, xc, xc + n)
-        op("p", lambda e, q: e.matmul_mx(ap(o), ap(a), ap(sa), ap(b), ap(sb), True, True), [a, sa, b, sb], [o], 1.3 * CYCLE * (n + 16))
+        op("p", lambda e, q: e.matmul_mx(ap(o), ap(a), ap(sa), ap(b), ap(sb), True, True), [a, sa, b, sb], [o], key)
 
     def bank(i, n, p0=0, p1=128, c0=0):
         return view("ps", 512 * i + c0, 512 * i + c0 + n, p0, p1)
 
-    def load(q, name, dst, n, sem, more=0.0):
+    def load(q, name, dst, n, rd=None):
         o = view(dst, 0, n)
-        op(q, lambda e, q: e.dma_start(ap(o), T[name][:, 0:n]), [], [o], 0.06, sem, 16, lag=LOCAL + more)
-        named("load." + name)
+        op(q, lambda e, q: e.dma_start(ap(o), T[name][:, 0:n]), [rd], [o], "load." + name, "d" + name, 16)
 
     def store(fn, i, sem):
-        op("ys", lambda e, q: fn(e), [i], [], 0.06, sem, 16, lag=LOCAL)
-        named("store." + sem)
-
-    def move(q, dst, d0, src, s0, n, s1, s2):
-        o, i, os, is_ = view(dst, d0, d0 + n), view(src, s0, s0 + n), view("s" + dst, d0, d0 + n), view("s" + src, s0, s0 + n)
-        op(q, lambda e, q: e.dma_start(ap(o).bitcast(dt.uint8), ap(i).bitcast(dt.uint8)), [i], [o], 0.06, s1, 16, lag=LOCAL)
-        named(s1)
-        op(q, lambda e, q: e.dma_start(ap(os), ap(is_)), [is_], [os], 0.06, s2, 16, lag=LOCAL)
-        named(s2)
+        op("ys", lambda e, q: fn(e), [i], [], "store." + sem, sem, 16)
 
     others = [d for d in range(N) if d != r]
-    where = [topo.addr(T.cores[d], core) for d in others]
     mask = topo.mask(core, T.cores[others[0]])
     for d in others:
         mask &= topo.mask(core, T.cores[d])
     lanes = bin(mask).count("1")
 
     def to_all(src, land, c0, k, sem):
-        dsts = []
-        for d in others:
-            j = r if r < d else r - 1
-            dsts.append(T[land][:, c0 + k * j:c0 + k * j + k])
-        tr = RemoteDMATransfer(dst_ids=[DstId(rid=int(a), pnc=int(b)) for a, b in where], dma_engine_mask=mask,
-                               remote_sem=T.sem[sem], srcs=[ap(src)], dsts=dsts, alu_op=0)
-        op("q", lambda e, q: e.remote_dma_fused([tr], local_sem=T.sem.left), [src], [], 1.0, "left", lanes, False, FLY)
-        named("send." + sem)
+        tr = RemoteDMATransfer(dst_ids=[DstId(rid=int(a), pnc=int(b)) for a, b in [topo.addr(T.cores[d], core) for d in others]],
+                               dma_engine_mask=mask, remote_sem=T.sem[sem], srcs=[ap(src)],
+                               dsts=[T[land][:, c0(j):c0(j) + k] for j in [r if r < d else r - 1 for d in others]], alu_op=0)
+        op("q", lambda e, q: e.remote_dma_fused([tr], local_sem=T.sem.left), [src], [], "send." + sem, "left", lanes, False)
 
     def to_one(d, d0, s0, n, parts, key=None):
         rid, pid = topo.addr(T.cores[d], core)
@@ -332,36 +269,33 @@ def rank_program(g, core, T, topo):
         c, s = view("SRC", s0, s0 + n), view("sSRC", s0, s0 + n)
         oc, os = T.SRC[:, d0:d0 + n].bitcast(dt.uint8), T.sSRC[:, d0:d0 + n]
         if "c" in parts:
-            op("q", lambda e, q: e.remote_dma(oc, ap(c).bitcast(dt.uint8), T.sem.halo, T.sem.left, pid, rid, m), [c], [], 0.7, "left", ln, False, FLY)
-            named("codes.%d" % (d > r))
+            op("q", lambda e, q: e.remote_dma(oc, ap(c).bitcast(dt.uint8), T.sem.halo, T.sem.left, pid, rid, m), [c], [], "codes.%d" % (d > r), "left", ln, False)
         if "s" in parts:
-            op("q", lambda e, q: e.remote_dma(os, ap(s), T.sem.halo, T.sem.left, pid, rid, m), [s], [], 0.7, "left", ln, False, FLY)
-            named(key or "scales.%d" % (d > r))
+            op("q", lambda e, q: e.remote_dma(os, ap(s), T.sem.halo, T.sem.left, pid, rid, m), [s], [], key or "scales.%d" % (d > r), "left", ln, False)
 
     def arrive(sem, n, writes):
-        ops.append({"qs": "", "fn": None, "rd": [], "wr": writes, "cost": 0.0, "sem": sem, "inc": n, "local": False, "lag": 0.0,
-                    "behind": max(k for k, o in enumerate(ops) if o["sem"] == "left"), "key": "come." + sem})
+        op("", None, [], writes, "come." + sem, sem, n, False)
+        ops[-1]["behind"] = max(k for k, o in enumerate(ops) if o["sem"] == "left")
 
-    load("s", "u", "U0", 8, "du")
-    load("y", "x", "XT", 4 * P, "dx", 0.0)
-    load("y", "a", "AT", 2048, "da", 2.0)
-    load("s", "b", "BT", 2048, "db", 2.0)
-    load("y", "w", "WT", 512, "dw", 2.0)
-    op("q", lambda e, q: e.iota(T.PI[:], [[0, 1]], 0, 1), [], [view("PI")], 0.16)
-    op("q", lambda e, q: e.iota(T.FI[:], [[1, 96]], 0, 0, allow_small_or_imprecise_dtypes=True), [], [view("FI")], 0.37)
+    load("s", "u", "U0", 8)
+    load("y", "x", "XT", 4 * P)
+    load("y", "a", "AT", 2048)
+    load("y", "b", "BT", 2048)
+    op("q", lambda e, q: e.iota(T.PI[:], [[0, 1]], 0, 1), [], [view("PI")])
+    op("q", lambda e, q: e.iota(T.FI[:], [[1, 96]], 0, 0, allow_small_or_imprecise_dtypes=True), [], [view("FI")])
     fill(view("Z32"), 0.0)
     fill(view("ZB"), 0.0)
     fill(view("U0", 8, 512), 0.0)
     fill(view("XT", 4 * P, 512), 0.0)
-    op("v", lambda e, q: e.tensor_scalar(T.PM[:, 0:1], T.PI[:], 31, None, AluOpType.bitwise_and), [view("PI")], [view("PM", 0, 1)], time(1))
-    op("v", lambda e, q: e.tensor_scalar(T.PM[:, 1:2], T.PI[:], 15, None, AluOpType.bitwise_and), [view("PI")], [view("PM", 1, 2)], time(1))
+    ts(view("PM", 0, 1), view("PI"), 31, AluOpType.bitwise_and)
+    ts(view("PM", 1, 2), view("PI"), 15, AluOpType.bitwise_and)
     copy(view("PF"), view("PI"), qs="v")
     copy(view("X32"), view("PM", 0, 1), qs="v")
     copy(view("X16"), view("PM", 1, 2), qs="v")
     tt(view("PA"), view("PF"), view("X32"), SUB)
     tt(view("XA"), view("X32"), view("PA"), SUB)
     tt(view("PB"), view("PA"), view("X16"), ADD)
-    alpha, beta, sigma = (BA - 1, BB, 2, 2), (AA, AB - 2, 1, 1), (1, 3, 1, 2)
+    alpha, beta, sigma = (BA - 1, 2, BB, 2), (AA, 1, AB - 2, 1), (1, 1, 3, 2)
     for a in range(4):
         for buf, c, v in (("KAP", 0, (4.0 * P * r + sigma[a]) * UNIT), ("FC", 0, MA * (129.0 - 0.5 * sigma[a]) + 2.0 * P * alpha[a]),
                           ("FC", 1, MB * (129.0 - 0.5 * sigma[a]) - 2.0 * P * beta[a]), ("WC", 0, 2.0 * P * alpha[a]), ("WC", 1, float(sigma[a]))):
@@ -376,26 +310,27 @@ def rank_program(g, core, T, topo):
     quant("QU", 0, 128, "UT")
     mm(1, "QU", 0, "SRC", 0, 128)
     copy(view("SROW"), bank(1, 96))
-    up, down = (r + 1, H0, P - (56 - 8 * r), 56 - 8 * r), (r - 1, H0 + HN - 8 * r, 0, 8 * r)
+    up, down = (r + 1, H0 + (64 if r == N - 2 else 0), P - (56 - 8 * r), 56 - 8 * r), (r - 1, H0 + HN - 8 * r, 0, 8 * r)
     to_one(*(up if r < N - 1 else down), "s", "first")
-    to_all(view("X1S"), "X1L", 0, 1, "x1")
-    arrive("x1", 7 * lanes, [view("X1L")])
+    at1 = [0, 128, 256, 384, 512, 513, 514]
+    to_all(view("X1S"), "X1L", lambda j: at1[j], 1, "x1")
+    arrive("x1", 7 * lanes, [view("X1L", c, c + 1) for c in at1])
+    load("y", "w", "WT", 512, view("X1L", 0, 1))
     if r < N - 1:
         to_one(*up, "c")
     if r > 0:
         to_one(*down, "cs" if r < N - 1 else "c")
     land, cnt = [], 0
+    cut = H0 + (64 - 8 * r if r < N - 1 else HN)
     if r > 0:
-        land += [view("SRC", H0, H0 + 64 - 8 * r), view("sSRC", H0, H0 + 64 - 8 * r)]
+        land += [view("SRC", cut - 64 + 8 * r, cut), view("sSRC", cut - 64 + 8 * r, cut)]
         cnt += 2 * bin(topo.mask(T.cores[r - 1], core)).count("1")
     if r < N - 1:
-        land += [view("SRC", H0 + 64 - 8 * r, H0 + HN), view("sSRC", H0 + 64 - 8 * r, H0 + HN)]
+        land += [view("SRC", cut, H0 + HN), view("sSRC", cut, H0 + HN)]
         cnt += 2 * bin(topo.mask(T.cores[r + 1], core)).count("1")
     arrive("halo", cnt, land)
-    if r == 0:
-        move("y", "SRC", H0, "SRC", 0, 64, "w2", "w3")
-    if r == N - 1:
-        move("y", "SRC", H0 + 8, "SRC", 0, 64, "w2", "w3")
+    if r in (0, N - 1):
+        quant("SRC", H0 - 64, 128, "XT")
 
     turn(view("TS"), view("SROW"))
     for a in range(4):
@@ -416,86 +351,101 @@ def rank_program(g, core, T, topo):
         ts(view("OE", 32 * b, 32 * b + 32), view("SQ"), s, EQ)
         ts(view("CM", o + 224, o + 256), view("SQ"), s, GT)
         tt(view("CM", o + 256, o + 288), view("OE", 32 * b, 32 * b + 32), view("TRI", 32 * b, 32 * b + 32), MUL)
-    count("CN", 288, view("CM", 800, 864), 32.0 * r)
-    copy(view("JC"), view("X32"))
-    ts(quarter("JC", 2), quarter("X32", 2), 32.0, ADD)
+    count("CN", 288, view("CM", 800, 864))
+    ts(view("JR", 0, 32), view("FI", 0, 32), view("PA"), ADD)
+    ts(view("JR", 32, 64), view("FI", 0, 32), view("PA"), ADD, -1.0, MUL)
     ts(view("KV"), view("FI"), 4.0 * UNIT, MUL, view("KAP"), ADD)
-    fill(quarter("VR", 3), -HUGE)
-    copy(quarter("VR", 2), quarter("SROW", 2))
+    fill(quarter("XS", 3), 0.0)
+    copy(quarter("VR", 1), quarter("SROW", 1))
+    for c in (0, 384):
+        ts(view("KT", c, c + 384), view("KT", c, c + 384), TOP, MIN, -TOP, MAX, "top.%d" % c)
     quant("SRC", P, 2 * P, "KT")
     mm(0, "QU", 0, "SRC", P, 2 * P)
     copy(quarter("VR", 0), bank(0, 96, 0, 32))
-    copy(quarter("VR", 1), bank(0, 96, 32, 64, 96))
+    copy(quarter("VR", 2), bank(0, 96, 64, 96, 96))
 
-    for i in range(4):
-        mm(1 + i, "QA", 128 * i, "SRC", P, 2 * P + HN)
-    for i in range(4):
-        mm((5 + i) % 8, "QB", 128 * i, "SRC", P, 2 * P + HN)
     fill(view("HK", 4 * HN, 4 * P), 0.0)
-    for i in range(8):
-        e0 = 4 * P * (i // 4)
-        copy(view("HK", e0 + i % 4, e0 + 4 * HN, step=4), bank((1 + i) % 8, HN, c0=2 * P), 0.0625)
-    for i in range(8):
-        e0 = 768 * (i // 4)
-        copy(view("GO", e0 + i % 4, e0 + 768, step=4), bank((1 + i) % 8, 2 * P), 0.0625)
-    quant("SRC", H0 + P, P + HN, "HK")
+    quant("QW", 0, 128, "WT")
+    parts = ((0, H0 + HN), (H0 + P, P + HN), (AA * P, 2 * P), (H0 + AA * P, P + HN), (BA * P, 2 * P), (H0 + BA * P, P + HN))
+    for (c0, w), (c1, _) in zip(parts, parts[1:]):
+        fill(view("YS", c0 + w, c1), 0.0)
+    for x in SEQ.split():
+        kind, i, bk = x[0], int(x[1]), int(x[2:] or 0)
+        if kind == "q":
+            if i == 1:
+                for c in (0, 384):
+                    ts(view("HK", c, c + 288), view("HK", c, c + 288), TOP, MIN, -TOP, MAX, "hop.%d" % c)
+            quant("SRC", *parts[i], *((), ("HK",), ("GO",), ("HG",), ("GO", 768), ("HG", 672))[i])
+            continue
+        if kind == "Y":
+            c0, w = parts[i]
+            mm(bk, "QW", 0, "SRC", c0, w, "mY%d" % i)
+            for c in range(0, w, 192):
+                copy(view("YS", c0 + c, c0 + min(w, c + 192)), bank(bk, min(w - c, 192), c0=c))
+            continue
+        c0, w = {"C": (P, 2 * P + HN), "H": (H0 + P, P + HN)}[kind]
+        mm(bk, "QA" if i < 4 else "QB", 128 * (i % 4), "SRC", c0, w, "m" + x[:2])
+        if kind == "C":
+            copy(view("HK", 4 * P * (i // 4) + i % 4, 4 * P * (i // 4) + 4 * HN, step=4), bank(bk, HN, c0=w - HN), 0.0625)
+            copy(view("GO", 768 * (i // 4) + i % 4, 768 * (i // 4) + 768, step=4), bank(bk, 2 * P), 0.0625)
+        else:
+            copy(view("HG", 672 * (i // 4) + i % 4, 672 * (i // 4) + 672, step=4), bank(bk, P + HN), 0.0625)
 
-    for j in range(N - 1):
-        spread(view("EX1", 32 * j, 32 * j + 32), view("X1L", j, j + 1))
-    turn(view("R1"), view("EX1"))
+    fill(view("MK"), 1.0)
+    fill(view("MK", 0, 64, step=32), 0.0)
+    for j in range(4):
+        fill(view("X1L", 128 * j + 4, 128 * j + 128, step=4), 0.0)
+    for j in (0, 2):
+        scan(view("EX1", 32 * j, 32 * j + 64), view("MK"), view("X1L", 128 * j, 128 * j + 256, step=4), 0.0, ADD, MUL)
+        turn(view("R1", 32 * j, 32 * j + 64), view("EX1", 32 * j, 32 * j + 64))
+    for j in range(4, N - 1):
+        spread(view("EX1", 32 * j, 32 * j + 32), view("X1L", at1[j], at1[j] + 1))
+    turn(view("R1", 128, 224), view("EX1", 128, 224))
     for b in range(2):
         s, o = view("TS", 32 * b, 32 * b + 1), 288 * b
         if r > 0:
-            ts(view("CM", o, o + 32 * r), view("R1", 0, 32 * r), s, GE)
-            named("GE.%d" % b)
+            ts(view("CM", o, o + 32 * r), view("R1", 0, 32 * r), s, GE, key="GE.%d" % b)
         if r < N - 1:
-            ts(view("CM", o + 32 * r, o + 224), view("R1", 32 * r, 224), s, GT)
-            named("GT.%d" % b)
+            ts(view("CM", o + 32 * r, o + 224), view("R1", 32 * r, 224), s, GT, key="GT.%d" % b)
         count("CN", 144 * b, view("CM", o, o + 288))
-    act(view("TG"), view("R1"), AF.Sign, bias=view("TS", 64, 65), scale=-1.0)
+    for c0, c1 in ((0, 128), (128, 224)):
+        act(view("TG", c0, c1), view("R1", c0, c1), AF.Sign, view("TS", 64, 65), -1.0)
+    ts(view("TG", 224, 225), view("CN", 319, 320), -1.0, MUL)
     if r > 0:
-        act(waste(view("TG", 0, 32 * r)), view("TG", 0, 32 * r), AF.Relu, acc=view("TA", 0, 1))
-        named("TA.0")
+        act(waste(view("TG", 0, 32 * r)), view("TG", 0, 32 * r), AF.Sign, 1.0, -1.0, view("TA", 0, 1), "TA.0")
     else:
         fill(view("TA", 0, 1), 0.0)
-    if r < N - 1:
-        act(waste(view("TG", 32 * r, 224)), view("TG", 32 * r, 224), AF.Relu, scale=-1.0, acc=view("TA", 1, 2))
-        named("TA.1")
-    else:
-        fill(view("TA", 1, 2), 0.0)
-    ts(view("CN", 431, 432), view("CN", 319, 320), view("TA", 0, 1), SUB, view("TA", 1, 2), ADD)
+    act(waste(view("TG", 32 * r, 225)), view("TG", 32 * r, 225), AF.Relu, scale=-1.0, acc=view("TA", 1, 2), key="TA.1")
     for a in (0, 1):
-        copy(quarter("CA", a, 0, 3), quarter("CN", 1 - a, 143, 432, 144))
-        copy(quarter("CA", a, 3, 6), quarter("CN", 2, 143, 432, 144))
+        copy(quarter("CA", a, 0, 2), quarter("CN", 1 - a, 143, 288, 144))
+        copy(quarter("CA", a, 3, 5), quarter("CN", 2, 143, 288, 144), -1.0)
+        spread(quarter("CA", a, 2, 3), quarter("TA", 1 - a, 1, 2), quarter("TA", 1 - a, 0, 1))
+        spread(quarter("CA", a, 5, 6), quarter("TA", 2, 1, 2), quarter("TA", 2, 0, 1))
+    for b in range(2):
+        spread(half("E0", 0, 32 * b, 32 * b + 32), half("CN", 0, 144 * b + 143, 144 * b + 144), half("JR", 0, 32, 64))
+    ts(half("E0", 0, 64, 96), half("JR", 0, 0, 32), half("TA", 0, 0, 1), SUB, half("TA", 0, 1, 2), SUB)
     for b in range(3):
-        spread(half("E0", 0, 32 * b, 32 * b + 32), half("CN", 0, 144 * b + 143, 144 * b + 144))
-        ts(half("EX3", 0, 32 * b, 32 * b + 32), half("E0", 0, 32 * b, 32 * b + 32), half("CA", 0, b, b + 1), ADD,
-           half("CA", 0, 3 + b, 4 + b), ADD)
-    turn(half("PR", 0), half("EX3", 0))
-    turn(half("PR", 1), half("EX3", 0))
-    ts(view("OH"), view("PR"), view("JC"), EQ)
-    tt(view("M2"), view("OH"), view("KV"), MUL)
-    sums(view("XS", 1, 2), view("M2"))
-    tt(view("M1"), view("OH"), view("VR"), MUL)
-    sums(view("XS", 0, 1), view("M1"))
-    to_all(view("XS"), "X2L", 2, 2, "x2")
+        ts(half("EX3", 0, 32 * b, 32 * b + 32), half("E0", 0, 32 * b, 32 * b + 32), half("CA", 0, b, b + 1), ADD if b < 2 else SUB, half("CA", 0, 3 + b, 4 + b), EQ)
+    turn(half("OH", 0), half("EX3", 0))
+    turn(quarter("OH", 2), quarter("EX3", 0))
+    for k, row in ((0, "VR"), (1, "KV")):
+        scan(view("M1", 96 * k, 96 * k + 96, 0, 96), view(row, 0, 96, 0, 96), view("OH", 0, 96, 0, 96), 0.0, MUL)
+        sums(view("XS", k, k + 1, 0, 96), view("M1", 96 * k, 96 * k + 96, 0, 96))
+    to_all(view("XS"), "X2L", lambda j: 2 + 2 * j, 2, "x2")
     arrive("x2", 7 * lanes, [view("X2L", 2, 16)])
 
     fill(view("X2L", 18, 84), 0.0)
     copy(view("X2L", 16, 18), view("XS"))
-    for i in range(8):
-        mm((1 + i) % 8, "QA" if i < 4 else "QB", 128 * (i % 4), "SRC", H0 + P, P + HN)
-    quant("SRC", AA * P, 2 * P, "GO")
-    quant("SRC", BA * P, 2 * P, "GO", 768)
     for h in range(2):
         ts(view("PC", h, h + 1), view("PB"), 16.0 * h, ADD, E - 1.0, MIN)
     swap("WC", 2, True)
     fill(view("KK", 0, 32), MA)
     fill(view("KK", 32, 64), MB)
     for k, m in ((0, MA), (1, MB)):
-        for j in (0, 1):
+        for j in range(2 - k, -1, -1)[1 - k:]:
+            n = 2 - k
             act(view("LH", 4 * k + 2 * j, 4 * k + 2 * j + 2), view("PC"), bias=2.0 * m * (E * r + j), scale=2.0 * m)
-    act(view("I0"), view("PC"), bias=-254.0 * E * r - 256.0 - 2.0 * P * r, scale=-254.0)
+    act(view("I0", 0, 1), view("PC", 0, 1), bias=-254.0 * E * r - 256.0 - 2.0 * P * r, scale=-254.0)
     act(view("P2"), view("PC"), bias=2.0 * E * r - 128.0 - 2.0 * P * r, scale=2.0)
     act(view("PN"), view("PC"), bias=2.0 * E * r - 128.0 - 2.0 * P * (r + 1), scale=2.0)
     act(view("H2"), view("PF"), bias=2.0 * MA * E * r, scale=2.0 * MA)
@@ -506,16 +456,10 @@ def rank_program(g, core, T, topo):
         fill(view("W", 128, 528, step=264), 0.0)
     if r == N - 1:
         fill(view("W", 260, 528, step=264), 0.0)
-    quant("QW", 0, 128, "WT")
-    for i in range(8):
-        e0 = 672 * (i // 4)
-        copy(view("HG", e0 + i % 4, e0 + 672, step=4), bank((1 + i) % 8, P + HN), 0.0625)
-    quant("SRC", H0 + AA * P, P + HN, "HG")
-    quant("SRC", H0 + BA * P, P + HN, "HG", 672)
 
-    sc, mc = view("EX2", 8, 9, 0, 96), view("EX2", 88, 89, 0, 96)
+    sc, mc = view("EX2", 8, 9, 0, 96), view("EX2", 144, 145, 0, 96)
     for k, row in ((0, "DS"), (1, "DN")):
-        c = 80 * k + 8
+        c = 136 * k + 8
         scan(view("EX2", c - 7, c + 32), view("X2L", 2 + k, 80 + k, step=2), view("X2L", 18, 57))
         turn(view(row, 0, 32, 0, 96), view("EX2", c, c + 32, 0, 96))
         for a in (0, 2):
@@ -523,19 +467,20 @@ def rank_program(g, core, T, topo):
             copy(quarter(row, a, 64, 96), quarter(row, 1, 0, 32))
         copy(quarter(row, 1, 32, 96), quarter(row, 0, 0, 64))
     ds, dn, sg, lo, bf = [view(x, 0, 96, 0, 96) for x in ("DS", "DN", "SG", "LO", "BF")]
-    act(sg, ds, AF.Sign, bias=sc, scale=-1.0)
+    act(sg, ds, AF.Sign, sc, -1.0)
     ts(lo, dn, mc, GE, -0.5, MUL)
     tt(bf, sg, lo, LE)
-    count("P1", 0, bf, 0.5 - K)
-    ts(view("EXM", 0, 32, 0, 96), view("Z32", 0, 32, 0, 96), view("P1", 47, 48, 0, 96), ADD, mc, MAX)
-    copy(quarter("EXM", 3), quarter("EX2", 3, 88, 120))
-    turn(view("MR", 0, 32), view("EXM"))
+    fill(view("BF", 96, 135), 0.0)
+    fill(view("EX2", 41, 137), -HUGE)
+    scan(view("EXM", 0, 135, 0, 96), view("BF", 0, 135, 0, 96), view("EX2", 41, 176, 0, 96), 0.5 - K, MAX)
+    ts(quarter("EXM", 3, 103, 135), quarter("EX2", 0, 144, 176), UNIT, ADD)
+    turn(view("MR", 0, 32), view("EXM", 103, 135))
     for h in (0, 1):
-        turn(half("MR", h, 32, 64), half("EXM", 1 - h))
+        turn(half("MR", h, 32, 64), half("EXM", 1 - h, 103, 135))
     swap("MR", 32)
-    signs(view("MR"), view("EXM", 0, 1), view("RK"), -1.0)
+    signs(view("MR"), view("EXM", 134, 135), view("RK"), -1.0)
     for k, m in ((0, MA), (1, MB)):
-        ts(view("F0", k, k + 1), view("EXM", 0, 1), 0.5 / UNIT * m, MUL, view("FC", k, k + 1), ADD)
+        ts(view("F0", k, k + 1), view("EXM", 134, 135), 0.5 / UNIT * m, MUL, view("FC", k, k + 1), ADD)
     if r > 0:
         signs(view("MR"), (4.0 * P * r - 0.5) * UNIT, view("SB", 0, 1), -1.0)
     if r < N - 1:
@@ -548,15 +493,20 @@ def rank_program(g, core, T, topo):
         swap(row, 32)
 
     if r > 0:
-        ts(view("W", 128, 528, step=264), view("P2"), view("SB", 0, 1), LT, 2.0 * (H0 + 64 - 8 * r), MUL)
-        named("low")
+        ts(view("W", 128, 528, step=264), view("P2"), view("SB", 0, 1), LT, 2.0 * cut, MUL, "low")
     if r < N - 1:
-        ts(view("W", 260, 528, step=264), view("PN"), view("SB", 1, 2), GE, -2.0 * (H0 - 32 - 8 * r), MUL)
-        named("high")
+        ts(view("W", 260, 528, step=264), view("PN"), view("SB", 1, 2), GE, -2.0 * (H0 - 32 - 8 * r), MUL, "high")
     for h in range(2):
         for k, row in ((0, "FR"), (1, "FB")):
             c = 264 * h + 132 * k
-            ts(view("W", c, c + 128), view(row), view("LH", 4 * k + h, 4 * k + h + 1), MAX, view("LH", 4 * k + 2 + h, 4 * k + 3 + h), MIN)
+            if h + k < 2:
+                ts(view("W", c, c + 128), view(row), view("LH", 4 * k + h, 4 * k + h + 1), MAX, view("LH", 4 * k + 2 + h, 4 * k + 3 + h), MIN)
+            else:
+                ts(view("W", c + 1, c + 128), view("ZB", 1, 128), view("LH", 1, 2), ADD)
+                act(view("W", c, c + 1), view("PC", 1, 2), bias=2.0 * MB * E * r + 256.0 + 2.0 * P * r + 256.0 * MB, scale=2.0 * MB)
+                act(view("NL"), view("PC", 1, 2), bias=-2.0 * MB * E * r, scale=-2.0 * MB)
+                act(view("TW"), view(row), AF.Relu, view("NL"))
+                act(waste(view("TW")), view("TW"), AF.Relu, 2.0 * MB, -1.0, view("I0", 1, 2), "I1")
         scan(view("OF", 130 * h, 130 * h + 129), view("W", 264 * h, 264 * h + 129), view("W", 264 * h + 132, 264 * h + 261), view("I0", h, h + 1), SUB)
     for a in range(4):
         for b in (a, a ^ 1):
@@ -565,13 +515,13 @@ def rank_program(g, core, T, topo):
         for h in (0, 1):
             ts(half("OT", d, 4 * h, 4 * h + 4), half("OTF", h, 4 * h, 4 * h + 4), 0.5, MUL)
     op("v", lambda e, q: e.tensor_copy(T.RUN[:, 0:128].bitcast(dt.uint32), T.SRC[:, 0:ALL].bitcast(dt.uint32).indirect(T.OT[:, 0:8])),
-       [view("SRC"), view("OT")], [view("RUN")], 0.26)
-    op("s", lambda e, q: e.activation(T.sRUN[:, 0:128], T.sSRC[:, 0:ALL].indirect(T.OT[:, 0:8]), AF.Copy),
-       [view("sSRC"), view("OT")], [view("sRUN")], 0.28)
+       [view("SRC"), view("OT")], [view("RUN")])
+    op("vs", lambda e, q: e.activation(T.sRUN[:, 0:128], T.sSRC[:, 0:ALL].indirect(T.OT[:, 0:8]), AF.Copy) if q == "s"
+       else e.tensor_copy(T.sRUN[:, 0:128], T.sSRC[:, 0:ALL].indirect(T.OT[:, 0:8])), [view("sSRC"), view("OT")], [view("sRUN")])
 
-    mm(0, "QW", 0, "RUN", 0, 128)
-    copy(view("YT"), bank(0, E))
-    store(lambda e: e.dma_start(T.y[:, 0:E], T.YT[:]), view("YT"), "o5")
+    op("vs", lambda e, q: e.tensor_copy(T.YT[:], T.YS[:].indirect(T.OT[:, 0:8])) if q == "v"
+       else e.activation(T.YT[:], T.YS[:].indirect(T.OT[:, 0:8]), AF.Copy), [view("YS"), view("OT")], [view("YT")])
+    store(lambda e: e.dma_start(T.y[:, 0:E], T.YT[:, 0:E]), view("YT"), "o5")
     store(lambda e: e.dma_start(T.oc[:, 0:4 * E], T.RUN[:, 0:E].bitcast(dt.uint8)), view("RUN", 0, E), "o0")
     for k in range(4):
         store(lambda e, k=k: e.dma_start(T.osc[4 * k:4 * k + 4, 0:E], T.sRUN[32 * k:32 * k + 4, 0:E]), view("sRUN", 0, E, 32 * k, 32 * k + 4), "o%d" % (1 + k))
@@ -583,10 +533,7 @@ def rank_program(g, core, T, topo):
     store(lambda e: e.dma_start(T.hs[0:1, 0:E], T.HB[0:E, 0:1]), view("HB", 0, 1, 0, E), "o6")
 
     order, queue = place(ops, *links(ops), ORDER)
-    total = {}
-    known = {k: {} for k in queues}
-    clocks = {}
-    log = {}
+    total, known, clocks, log = {}, {k: {} for k in queues}, {}, {}
 
     def await_(q, need):
         for s, n in sorted(need.items()):

from concourse.bass import DstId, RemoteDMATransfer
from concourse.mybir import dt, AluOpType, AxisListType, ActivationFunctionType

N, P, K = 8, 96, 32
E = P + 2 * K // N
AA, AB, BA, BB = 6, 7, 11, 12
H0 = 3 * P
HN = 72
ALL = H0 + BB * P + HN
MA, MB = 2049.0, 2048.0
SEQ = "C01 C12 C23 C34 C45 C56 C67 C70 Y01 q1 q2 q4 H02 H13 H24 H35 Y16 Y27 H40 H51 H62 H73 q3 q5 Y44 Y35 Y56"
TOP = 2.0 ** 31
UNIT = 2.0 ** -20
HUGE = 1.0e29
CODE = "float8_e4m3fn_x4"
HALF = "bfloat16"
ORDER = """
U0.0.8:v load.x:y MK.0.0:v load.u:s PI.0.0:q W.0.128:v Z32.0.0:v WC.2.0:s WC.3.1:s PM.0.0:v TA.0.0:v WC.2.1:s PF.0.0:v FC.1.1:s XT.0.384:v
WC.1.0:s ZB.0.0:v X1L.0.260:v X32.0.0:v XS.3.0:v X1L.0.4:v WC.1.1:s MK.0.0.2:v HK.0.288:v PA.0.0:v SRC.0.0:v UT.0.2:v WC.0.0:s UT.0.0:v
WC.0.1:s FC.3.0:s UT.0.3:v KAP.0.0:s UT.0.1:v KAP.2.0:s WC.3.0:s QV.0.0:v FI.0.0:q load.a:y WC.2.2:s XA.0.0:v X1L.0.132:v H2.0.0:s NH.0.0:s
QU.0.0:v ps.0.0:p X1L.0.388:v PM.0.1:v FC.1.0:s JR.0.0:v ps.0.512:p FC.2.0:s WC.0.2:s load.b:y FC.0.1:s XB.0.0:v WC.2.4:s FC.3.1:s FC.0.0:s
first:q KAP.1.0:s WC.1.4:s WC.0.4:s XB.0.1:v KAP.3.0:s XB.0.2:v WC.3.4:s X1S.0.0:s FC.2.1:s WH.0.128:s SROW.0.0:s QA.0.0:v SQ.3.0:s TRI.0.64:v
SQ.0.0:s send.x1:q ps.0.512.2:p SQ.2.0:s codes.1:q SQ.1.0:s TS.0.0:v ps.0.1024:p ps.0.0.2:p QB.0.0:v OE.0.64:v OE.0.32:v OE.0.0:v TRI.0.0:v
VR.1.0:s codes.0:q TRI.0.32:v KT.0.1:s CM.0.512:v KT.0.2:s KT.0.0:s CM.0.832:v ps.0.1536:p CM.0.800:v CM.0.224:v X16.0.0:v SRC.0.224:v
KT.0.3:s ps.0.3072:p ps.0.3584:p KT.0.386:s come.x1:- CM.0.544:v KT.0.387:s ps.0.2048:p ps.0.2560:p KT.0.384:s CN.0.288:v KT.0.385:s
EX1.0.192:s top.0:v EX1.0.128:s EX1.0.0:v CM.0.256:v EX1.0.64:v EX1.0.160:s TG.0.224:v R1.0.0:v scales.0:q top.384:v R1.0.64:v R1.0.128:v
TG.0.0:s SRC.0.96:v TG.0.128:s JR.0.32:v GE.0:v TA.0:s GT.0:v GE.1:v come.halo:- ps.0.0.3:p TA.1:s GT.1:v CN.0.0:v VR.0.0:s mC0:p CN.0.144:v
CA.1.5:s CA.1.2:v E0.0.64:v CA.0.2:s mC1:p E0.0.0:v CA.0.3:v CA.1.3:v CA.0.5:s X2L.0.18:v CA.0.0:s CA.1.0:s E0.0.32:s mC4:p PB.0.0:v mC2:p
EX3.0.64:v HK.0.0:s EX3.0.0:v EX3.0.32:v VR.2.0:s KV.0.0:v HK.0.1:s mC3:p GO.0.0:s mC5:p HK.0.384:s OH.2.0:v load.w:y OH.0.0:v PC.0.0:v
GO.0.1:s PC.0.1:v M1.0.0:v M1.0.96:v mC6:p XS.0.0:v GO.0.768:s XS.0.1:v send.x2:q HK.0.2:s NL.0.0:s mC7:p BF.0.96:v PN.0.0:s YS.0.360:v
LH.0.2:s H4.0.0:v LH.0.0:s YS.0.552:v HK.0.3:s KK.0.0:v GO.0.2:s come.x2:- HK.0.385:v QW.0.0:v X2L.0.16:s GO.0.3:s HK.0.386:s YS.0.1032:v
GO.0.769:s YS.0.768:v HK.0.387:s W.0.397:v KK.0.32:v GO.0.770:s hop.0:v SRC.0.576:v hop.384:v mY0:p LH.0.6:s YS.0.1248:v GO.0.771:s YS.0.0:s
W.0.396:s YS.0.192:s mY2:p SRC.0.384:v P2.0.0:s mH1:p mH0:p mH3:p I0.0.0:s YS.0.576:s SRC.0.1056:v EX2.0.1:v EX2.0.137:v mH2:p DS.0.0:v
DS.2.64:s mH5:p DS.0.32:v DN.0.0:v DS.1.32:s DN.0.32:v DS.2.32:v DN.0.64:s DS.0.64:v DN.2.32:v DN.2.64:s DN.1.32:v SG.0.0:s mH4:p HG.0.1:v
HG.0.0:s LO.0.0:v HG.0.3:s mH6:p EX2.0.41:v HG.0.2:s BF.0.0:v EXM.3.103:v EXM.0.0:v SRC.0.864:v MR.2.32:v MR.0.0:v MR.0.32:v mH7:p LH.0.4:s
HG.0.673:s HG.0.672:s HG.0.674:s MR.3.64:v MR.1.64:v HG.0.675:v F0.0.1:v MR.2.64:s MR.0.64:s sg.RK.0:s mY1:p F0.0.0:v YS.0.384:s EXF.0.64:s
EXF.0.0:s SRC.0.1344:v EXF.2.32:s EXF.2.96:v sg.SB.0:s EXF.0.96:v EXF.0.32:v mY4:p FB.0.0:v mY3:p sg.SB.1:s FR.0.0:v FB.2.64:s FB.3.64:s
FR.3.64:s FB.0.64:v FR.2.64:s FB.1.64:v FR.1.64:v low:v WH.0.0:v high:v W.0.132:v FR.0.64:s mY5:p TW.0.0:s I1:s W.0.0:v YS.0.1344:s W.0.264:v
OF.0.0:v OF.0.130:v WH.0.96:v WH.0.64:v WH.0.32:v YS.0.1056:s OTF.1.2:s OTF.0.0:s OTF.0.2:v OTF.2.4:s OTF.1.0:v OTF.3.4:v OTF.3.6:s
sg.WH.129:s OTF.2.6:v OT.0.0:v OT.2.0:v OT.0.4:v sg.WH.130:s OT.2.4:v YS.0.864:s HB.0.0:s YT.0.0:s RUN.0.0:v sRUN.0.0:v store.o6:y store.o0:y
store.o5:s store.o1:y store.o2:s store.o4:y store.o3:y
"""


def _sb(n, d="float32"):
    return ("sbuf", [128, n], d)


SCRATCH = {"ps": ("psum", [128, 4096], "float32")}
for _d, _l in ((HALF, "XT:512 U0:512 UT:512 ZB:128 AT:2048 BT:2048 WT:512 KT:768 GO:1536 HK:672 HG:1344 CM:864 CN:432 TG:226 SG:96 LO:96"),
               (CODE, "QU:128 QV:128 QA:512 QB:512 QW:128 SRC:%d RUN:128" % ALL), ("int32", "PI:1 PM:2"), ("uint16", "OT:8"),
               ("float32", "YT:128 YS:1512 Z32:32 PF:1 X32:1 X16:1 FI:96 JR:64 E0:96 XA:1 XB:3 TRI:96 KAP:1 KV:96 VR:96 FC:2 PA:1 PB:1 PC:2 P2:2 PN:2 "
                "H2:1 NH:1 WC:8 KK:64 LH:8 I0:2 H4:4 X1S:1 X1L:516 SROW:96 SQ:32 TS:96 OE:96 EX1:224 R1:224 CA:6 TA:2 MK:64 NL:1 TW:128 EX3:96 "
                "OH:96 M1:192 XS:2 X2L:84 EX2:176 BF:135 DS:96 DN:96 EXM:135 MR:128 F0:2 RK:1 SB:2 EXF:128 FR:128 FB:128 J4:2560 W:528 OF:260 "
                "OTF:8 WH:132 HB:1")):
    for _x in _l.split():
        SCRATCH[_x.split(":")[0]] = _sb(int(_x.split(":")[1]), _d)
        if _d == CODE:
            SCRATCH["s" + _x.split(":")[0]] = _sb(int(_x.split(":")[1]), "uint8")
SEMAPHORES = "v s p q dx du da db dw o0 o1 o2 o3 o4 o5 o6 x1 x2 halo left".split()
AF = ActivationFunctionType
ADD, SUB, MUL, MIN, MAX = AluOpType.add, AluOpType.subtract, AluOpType.mult, AluOpType.min, AluOpType.max
GT, GE, LT, LE, EQ = AluOpType.is_gt, AluOpType.is_ge, AluOpType.is_lt, AluOpType.is_le, AluOpType.is_equal


def view(name, c0=0, c1=None, p0=0, p1=128, step=1):
    return (name, p0, p1, c0, SCRATCH[name][1][1] if c1 is None else c1, step)


def quarter(name, a, c0=0, c1=None, step=1):
    return view(name, c0, c1, 32 * a, 32 * a + 32, step)


def half(name, h, c0=0, c1=None):
    return view(name, c0, c1, 64 * h, 64 * h + 64)


def width(w):
    return len(range(w[3], w[4], w[5]))


def meet(a, b):
    if a[1] >= b[2] or b[1] >= a[2] or a[3] >= b[4] or b[3] >= a[4]:
        return False
    return (a[5] == 1 and b[5] == 1) or bool(set(range(a[3], a[4], a[5])) & set(range(b[3], b[4], b[5])))


def holds(a, b):
    return a[5] == 1 and a[1] <= b[1] and a[2] >= b[2] and a[3] <= b[3] and a[4] >= b[4]


def wide(w):
    return w if w[0] != "ps" else ("ps", 0, 128, w[3] // 512 * 512, (w[4] + 511) // 512 * 512, 1)


def accesses(o):
    return [(w, False) for w in o["rd"]] + [(w, True) for w in o["wr"]]


def links(ops):
    log, before, last = {}, [set() for _ in ops], None
    for i, o in enumerate(ops):
        for w, wr in accesses(o):
            for v, vr, j in log.get(w[0], []):
                if j != i and (wr or vr or w[0] == "ps") and meet(wide(w), v):
                    before[i].add(j)
        if "behind" in o:
            before[i].add(o["behind"])
        if o["qs"] == "q":
            if last is not None:
                before[i].add(last)
            last = i
        for w, wr in accesses(o):
            w = wide(w)
            l = log.setdefault(w[0], [])
            if wr:
                l[:] = [e for e in l if e[2] == i or not holds(w, e[0])]
            l.append((w, wr, i))
    keys, seen = [], {}
    for o in ops:
        w = (o["wr"] or o["rd"])[0]
        k = o.get("key") or "%s.%d.%d" % (w[0], w[1] // 32, w[3])
        seen[k] = seen.get(k, 0) + 1
        keys.append(k if seen[k] == 1 else "%s.%d" % (k, seen[k]))
    return before, keys


def place(ops, before, keys, table):
    n = len(ops)
    after = [[] for _ in ops]
    for i in range(n):
        for j in before[i]:
            after[j].append(i)
    missing = [len(b) for b in before]
    ready = [i for i in range(n) if missing[i] == 0]
    queue, rank = [""] * n, {}
    for k, x in enumerate(table.split()):
        x = x.split(":")
        rank[x[0]] = (float(k), x[1])
    at, order = [0.0] * n, []
    for i in range(n):
        at[i], queue[i] = rank.get(keys[i], (max([at[j] for j in before[i]], default=0.0) + 0.5, "-"))
        if queue[i] not in ops[i]["qs"]:
            queue[i] = ops[i]["qs"][:1] or "-"
    while ready:
        i = min(ready, key=lambda k: (at[k], k))
        ready.remove(i)
        order.append(i)
        for k in after[i]:
            missing[k] -= 1
            if missing[k] == 0:
                ready.append(k)
    return order, queue


def rank_program(g, core, T, topo):
    r = T.rank_of(core)
    if r is None:
        return
    queues = {"v": g.vector, "s": g.scalar, "p": g.tensor, "q": g, "y": g.sync}
    ops = []

    def ap(w):
        n, p0, p1, c0, c1, st = w
        return T[n][p0:p1, c0:c1] if st == 1 else T[n][p0:p1, c0:c1:st]

    def op(qs, fn, reads, writes, key=None, sem=None, inc=1, local=True):
        ops.append({"qs": qs, "fn": fn, "rd": [x for x in reads if isinstance(x, tuple)], "wr": writes, "sem": sem, "inc": inc, "local": local, "key": key})

    def val(x):
        return ap(x) if isinstance(x, tuple) else x

    def act(o, i, func=AF.Copy, bias=None, scale=None, acc=None, key=None):
        kw = {k: val(x) for k, x in (("bias", bias), ("scale", scale), ("accum_out", acc)) if x is not None}
        op("s", lambda e, q: e.activation(ap(o), ap(i), func, **kw), [i, bias, scale], [o] + ([acc] if acc else []), key)

    def ts(o, i, s1, op0, s2=None, op1=None, key=None):
        op("v", lambda e, q: e.tensor_scalar(ap(o), ap(i), val(s1), val(s2), *([op0] if op1 is None else [op0, op1])), [i, s1, s2], [o], key)

    def copy(o, i, scale=None, qs="vs"):
        def fn(e, q):
            if q == "v":
                return e.tensor_copy(ap(o), ap(i)) if scale is None else e.tensor_scalar(ap(o), ap(i), scale, None, MUL)
            return e.activation(ap(o), ap(i), AF.Copy) if scale is None else e.activation(ap(o), ap(i), AF.Copy, scale=scale)
        op(qs, fn, [i], [o])

    def spread(o, x, z=None):
        z = z or view("Z32", 0, 32, x[1], x[2])
        op("vs", lambda e, q: e.tensor_scalar(ap(o), ap(z), ap(x), None, ADD) if q == "v" else e.activation(ap(o), ap(z), AF.Identity, bias=ap(x)),
           [z, x], [o])

    def lay(o, z, x, y):
        op("vs", lambda e, q: e.tensor_scalar(ap(o), ap(z), ap(x), ap(y), MUL, ADD) if q == "v"
           else e.activation(ap(o), ap(z), AF.Identity, bias=ap(y), scale=ap(x)), [z, x, y], [o])

    junk = [0]

    def waste(i):
        junk[0] += width(i)
        return view("J4", junk[0] - width(i), junk[0], i[1], i[2])

    def sums(o, i):
        j = waste(i)
        op("vs", lambda e, q: e.tensor_reduce(ap(o), ap(i), AxisListType.X, ADD) if q == "v"
           else e.activation(ap(j), ap(i), AF.Copy, accum_out=ap(o)), [i], [o, j])

    def scan(o, x, y, first=0.0, op1=ADD, op0=ADD):
        op("v", lambda e, q: e.tensor_tensor_scan(ap(o), ap(x), ap(y), val(first), op0, op1), [x, y, first], [o])

    def count(name, c0, i, first=0.0):
        n, p0, p1, a, b, _ = i
        m = (a + b) // 2
        scan(view(name, c0, c0 + m - a, p0, p1), view(n, a, m, p0, p1), view(n, m, b, p0, p1), first)

    def signs(i, bias, acc, scale=1.0):
        act(waste(i), i, AF.Sign, bias, scale, acc, "sg.%s.%d" % (acc[0], acc[3]))

    def tt(o, a, b, o0):
        op("v", lambda e, q: e.tensor_tensor(ap(o), ap(a), ap(b), o0), [a, b], [o])

    def fill(o, c):
        op("v", lambda e, q: e.memset(ap(o), c), [], [o])

    def turn(o, i):
        op("v", lambda e, q: e.transpose(ap(o), ap(i)), [i], [o])

    def swap(name, n, both=False):
        if both:
            for h in (0, 1):
                copy(half(name, h, n, 2 * n), half(name, 1 - h, 0, n))
        for a in range(4):
            copy(quarter(name, a, 2 * n, 4 * n), quarter(name, a ^ 1, 0, 2 * n))

    def quant(dst, c0, n, src, e0=0):
        o, s, i = view(dst, c0, c0 + n), view("s" + dst, c0, c0 + n), view(src, e0, e0 + 4 * n)
        op("v", lambda e, q: e.quantize_mx(ap(o), ap(s), ap(i)), [i], [o, s])

    def mm(bk, w, wc, x, xc, n, key=None):
        o = view("ps", 512 * bk, 512 * bk + n)
        a, sa, b, sb = view(w, wc, wc + 128), view("s" + w, wc, wc + 128), view(x, xc, xc + n), view("s" + x, xc, xc + n)
        op("p", lambda e, q: e.matmul_mx(ap(o), ap(a), ap(sa), ap(b), ap(sb), True, True), [a, sa, b, sb], [o], key)

    def bank(i, n, p0=0, p1=128, c0=0):
        return view("ps", 512 * i + c0, 512 * i + c0 + n, p0, p1)

    def load(q, name, dst, n, rd=None):
        o = view(dst, 0, n)
        op(q, lambda e, q: e.dma_start(ap(o), T[name][:, 0:n]), [rd], [o], "load." + name, "d" + name, 16)

    def store(fn, i, sem):
        op("ys", lambda e, q: fn(e), [i], [], "store." + sem, sem, 16)

    others = [d for d in range(N) if d != r]
    mask = topo.mask(core, T.cores[others[0]])
    for d in others:
        mask &= topo.mask(core, T.cores[d])
    lanes = bin(mask).count("1")

    def to_all(src, land, c0, k, sem):
        tr = RemoteDMATransfer(dst_ids=[DstId(rid=int(a), pnc=int(b)) for a, b in [topo.addr(T.cores[d], core) for d in others]],
                               dma_engine_mask=mask, remote_sem=T.sem[sem], srcs=[ap(src)],
                               dsts=[T[land][:, c0(j):c0(j) + k] for j in [r if r < d else r - 1 for d in others]], alu_op=0)
        op("q", lambda e, q: e.remote_dma_fused([tr], local_sem=T.sem.left), [src], [], "send." + sem, "left", lanes, False)

    def to_one(d, d0, s0, n, parts, key=None):
        rid, pid = topo.addr(T.cores[d], core)
        m = topo.mask(core, T.cores[d])
        ln = bin(m).count("1")
        c, s = view("SRC", s0, s0 + n), view("sSRC", s0, s0 + n)
        oc, os = T.SRC[:, d0:d0 + n].bitcast(dt.uint8), T.sSRC[:, d0:d0 + n]
        if "c" in parts:
            op("q", lambda e, q: e.remote_dma(oc, ap(c).bitcast(dt.uint8), T.sem.halo, T.sem.left, pid, rid, m), [c], [], "codes.%d" % (d > r), "left", ln, False)
        if "s" in parts:
            op("q", lambda e, q: e.remote_dma(os, ap(s), T.sem.halo, T.sem.left, pid, rid, m), [s], [], key or "scales.%d" % (d > r), "left", ln, False)

    def arrive(sem, n, writes):
        op("", None, [], writes, "come." + sem, sem, n, False)
        ops[-1]["behind"] = max(k for k, o in enumerate(ops) if o["sem"] == "left")

    load("s", "u", "U0", 8)
    load("y", "x", "XT", 4 * P)
    load("y", "a", "AT", 2048)
    load("y", "b", "BT", 2048)
    op("q", lambda e, q: e.iota(T.PI[:], [[0, 1]], 0, 1), [], [view("PI")])
    op("q", lambda e, q: e.iota(T.FI[:], [[1, 96]], 0, 0, allow_small_or_imprecise_dtypes=True), [], [view("FI")])
    fill(view("Z32"), 0.0)
    fill(view("ZB"), 0.0)
    fill(view("U0", 8, 512), 0.0)
    fill(view("XT", 4 * P, 512), 0.0)
    ts(view("PM", 0, 1), view("PI"), 31, AluOpType.bitwise_and)
    ts(view("PM", 1, 2), view("PI"), 15, AluOpType.bitwise_and)
    copy(view("PF"), view("PI"), qs="v")
    copy(view("X32"), view("PM", 0, 1), qs="v")
    copy(view("X16"), view("PM", 1, 2), qs="v")
    tt(view("PA"), view("PF"), view("X32"), SUB)
    tt(view("XA"), view("X32"), view("PA"), SUB)
    tt(view("PB"), view("PA"), view("X16"), ADD)
    alpha, beta, sigma = (BA - 1, 2, BB, 2), (AA, 1, AB - 2, 1), (1, 1, 3, 2)
    for a in range(4):
        for buf, c, v in (("KAP", 0, (4.0 * P * r + sigma[a]) * UNIT), ("FC", 0, MA * (129.0 - 0.5 * sigma[a]) + 2.0 * P * alpha[a]),
                          ("FC", 1, MB * (129.0 - 0.5 * sigma[a]) - 2.0 * P * beta[a]), ("WC", 0, 2.0 * P * alpha[a]), ("WC", 1, float(sigma[a]))):
            act(quarter(buf, a, c, c + 1), quarter("Z32", a, 0, 1), bias=v)
    quant("QV", 0, 128, "U0")
    quant("SRC", 0, 128, "XT")

    mm(0, "SRC", 0, "QV", 0, 128)
    copy(view("X1S"), bank(0, 1))
    for t in range(4):
        ts(view("UT", t, 512, step=4), view("ZB"), view("U0", t, t + 1), ADD)
    quant("QU", 0, 128, "UT")
    mm(1, "QU", 0, "SRC", 0, 128)
    copy(view("SROW"), bank(1, 96))
    up, down = (r + 1, H0 + (64 if r == N - 2 else 0), P - (56 - 8 * r), 56 - 8 * r), (r - 1, H0 + HN - 8 * r, 0, 8 * r)
    to_one(*(up if r < N - 1 else down), "s", "first")
    at1 = [0, 128, 256, 384, 512, 513, 514]
    to_all(view("X1S"), "X1L", lambda j: at1[j], 1, "x1")
    arrive("x1", 7 * lanes, [view("X1L", c, c + 1) for c in at1])
    load("y", "w", "WT", 512, view("X1L", 0, 1))
    if r < N - 1:
        to_one(*up, "c")
    if r > 0:
        to_one(*down, "cs" if r < N - 1 else "c")
    land, cnt = [], 0
    cut = H0 + (64 - 8 * r if r < N - 1 else HN)
    if r > 0:
        land += [view("SRC", cut - 64 + 8 * r, cut), view("sSRC", cut - 64 + 8 * r, cut)]
        cnt += 2 * bin(topo.mask(T.cores[r - 1], core)).count("1")
    if r < N - 1:
        land += [view("SRC", cut, H0 + HN), view("sSRC", cut, H0 + HN)]
        cnt += 2 * bin(topo.mask(T.cores[r + 1], core)).count("1")
    arrive("halo", cnt, land)
    if r in (0, N - 1):
        quant("SRC", H0 - 64, 128, "XT")

    turn(view("TS"), view("SROW"))
    for a in range(4):
        copy(quarter("SQ", a), quarter("SROW", a, 32 * (a % 3), 32 * (a % 3) + 32))
    quant("QA", 0, 512, "AT")
    for i in range(4):
        mm(i, "QA", 128 * i, "SRC", 0, 128)
    quant("QB", 0, 512, "BT")
    for i in range(4):
        mm(4 + i, "QB", 128 * i, "SRC", 0, 128)
    for i in range(8):
        copy(view("KT", i % 4 + 384 * (i // 4), 384 + 384 * (i // 4), step=4), bank(i, 96), 0.0625)
    for b in range(3):
        ts(view("XB", b, b + 1), view("XA"), 32.0 * b, ADD)
    for b in range(3):
        s, o = view("TS", 32 * b, 32 * b + 1), 288 * b
        ts(view("TRI", 32 * b, 32 * b + 32), view("FI", 0, 32), view("XB", b, b + 1), LT)
        ts(view("OE", 32 * b, 32 * b + 32), view("SQ"), s, EQ)
        ts(view("CM", o + 224, o + 256), view("SQ"), s, GT)
        tt(view("CM", o + 256, o + 288), view("OE", 32 * b, 32 * b + 32), view("TRI", 32 * b, 32 * b + 32), MUL)
    count("CN", 288, view("CM", 800, 864))
    ts(view("JR", 0, 32), view("FI", 0, 32), view("PA"), ADD)
    ts(view("JR", 32, 64), view("FI", 0, 32), view("PA"), ADD, -1.0, MUL)
    ts(view("KV"), view("FI"), 4.0 * UNIT, MUL, view("KAP"), ADD)
    fill(quarter("XS", 3), 0.0)
    copy(quarter("VR", 1), quarter("SROW", 1))
    for c in (0, 384):
        ts(view("KT", c, c + 384), view("KT", c, c + 384), TOP, MIN, -TOP, MAX, "top.%d" % c)
    quant("SRC", P, 2 * P, "KT")
    mm(0, "QU", 0, "SRC", P, 2 * P)
    copy(quarter("VR", 0), bank(0, 96, 0, 32))
    copy(quarter("VR", 2), bank(0, 96, 64, 96, 96))

    fill(view("HK", 4 * HN, 4 * P), 0.0)
    quant("QW", 0, 128, "WT")
    parts = ((0, H0 + HN), (H0 + P, P + HN), (AA * P, 2 * P), (H0 + AA * P, P + HN), (BA * P, 2 * P), (H0 + BA * P, P + HN))
    for (c0, w), (c1, _) in zip(parts, parts[1:]):
        fill(view("YS", c0 + w, c1), 0.0)
    for x in SEQ.split():
        kind, i, bk = x[0], int(x[1]), int(x[2:] or 0)
        if kind == "q":
            if i == 1:
                for c in (0, 384):
                    ts(view("HK", c, c + 288), view("HK", c, c + 288), TOP, MIN, -TOP, MAX, "hop.%d" % c)
            quant("SRC", *parts[i], *((), ("HK",), ("GO",), ("HG",), ("GO", 768), ("HG", 672))[i])
            continue
        if kind == "Y":
            c0, w = parts[i]
            mm(bk, "QW", 0, "SRC", c0, w, "mY%d" % i)
            for c in range(0, w, 192):
                copy(view("YS", c0 + c, c0 + min(w, c + 192)), bank(bk, min(w - c, 192), c0=c))
            continue
        c0, w = {"C": (P, 2 * P + HN), "H": (H0 + P, P + HN)}[kind]
        mm(bk, "QA" if i < 4 else "QB", 128 * (i % 4), "SRC", c0, w, "m" + x[:2])
        if kind == "C":
            copy(view("HK", 4 * P * (i // 4) + i % 4, 4 * P * (i // 4) + 4 * HN, step=4), bank(bk, HN, c0=w - HN), 0.0625)
            copy(view("GO", 768 * (i // 4) + i % 4, 768 * (i // 4) + 768, step=4), bank(bk, 2 * P), 0.0625)
        else:
            copy(view("HG", 672 * (i // 4) + i % 4, 672 * (i // 4) + 672, step=4), bank(bk, P + HN), 0.0625)

    fill(view("MK"), 1.0)
    fill(view("MK", 0, 64, step=32), 0.0)
    for j in range(4):
        fill(view("X1L", 128 * j + 4, 128 * j + 128, step=4), 0.0)
    for j in (0, 2):
        scan(view("EX1", 32 * j, 32 * j + 64), view("MK"), view("X1L", 128 * j, 128 * j + 256, step=4), 0.0, ADD, MUL)
        turn(view("R1", 32 * j, 32 * j + 64), view("EX1", 32 * j, 32 * j + 64))
    for j in range(4, N - 1):
        spread(view("EX1", 32 * j, 32 * j + 32), view("X1L", at1[j], at1[j] + 1))
    turn(view("R1", 128, 224), view("EX1", 128, 224))
    for b in range(2):
        s, o = view("TS", 32 * b, 32 * b + 1), 288 * b
        if r > 0:
            ts(view("CM", o, o + 32 * r), view("R1", 0, 32 * r), s, GE, key="GE.%d" % b)
        if r < N - 1:
            ts(view("CM", o + 32 * r, o + 224), view("R1", 32 * r, 224), s, GT, key="GT.%d" % b)
        count("CN", 144 * b, view("CM", o, o + 288))
    for c0, c1 in ((0, 128), (128, 224)):
        act(view("TG", c0, c1), view("R1", c0, c1), AF.Sign, view("TS", 64, 65), -1.0)
    ts(view("TG", 224, 225), view("CN", 319, 320), -1.0, MUL)
    if r > 0:
        act(waste(view("TG", 0, 32 * r)), view("TG", 0, 32 * r), AF.Sign, 1.0, -1.0, view("TA", 0, 1), "TA.0")
    else:
        fill(view("TA", 0, 1), 0.0)
    act(waste(view("TG", 32 * r, 225)), view("TG", 32 * r, 225), AF.Relu, scale=-1.0, acc=view("TA", 1, 2), key="TA.1")
    for a in (0, 1):
        copy(quarter("CA", a, 0, 2), quarter("CN", 1 - a, 143, 288, 144))
        copy(quarter("CA", a, 3, 5), quarter("CN", 2, 143, 288, 144), -1.0)
        spread(quarter("CA", a, 2, 3), quarter("TA", 1 - a, 1, 2), quarter("TA", 1 - a, 0, 1))
        spread(quarter("CA", a, 5, 6), quarter("TA", 2, 1, 2), quarter("TA", 2, 0, 1))
    for b in range(2):
        spread(half("E0", 0, 32 * b, 32 * b + 32), half("CN", 0, 144 * b + 143, 144 * b + 144), half("JR", 0, 32, 64))
    ts(half("E0", 0, 64, 96), half("JR", 0, 0, 32), half("TA", 0, 0, 1), SUB, half("TA", 0, 1, 2), SUB)
    for b in range(3):
        ts(half("EX3", 0, 32 * b, 32 * b + 32), half("E0", 0, 32 * b, 32 * b + 32), half("CA", 0, b, b + 1), ADD if b < 2 else SUB, half("CA", 0, 3 + b, 4 + b), EQ)
    turn(half("OH", 0), half("EX3", 0))
    turn(quarter("OH", 2), quarter("EX3", 0))
    for k, row in ((0, "VR"), (1, "KV")):
        scan(view("M1", 96 * k, 96 * k + 96, 0, 96), view(row, 0, 96, 0, 96), view("OH", 0, 96, 0, 96), 0.0, MUL)
        sums(view("XS", k, k + 1, 0, 96), view("M1", 96 * k, 96 * k + 96, 0, 96))
    to_all(view("XS"), "X2L", lambda j: 2 + 2 * j, 2, "x2")
    arrive("x2", 7 * lanes, [view("X2L", 2, 16)])

    fill(view("X2L", 18, 84), 0.0)
    copy(view("X2L", 16, 18), view("XS"))
    for h in range(2):
        ts(view("PC", h, h + 1), view("PB"), 16.0 * h, ADD, E - 1.0, MIN)
    swap("WC", 2, True)
    fill(view("KK", 0, 32), MA)
    fill(view("KK", 32, 64), MB)
    for k, m in ((0, MA), (1, MB)):
        for j in range(2 - k, -1, -1)[1 - k:]:
            n = 2 - k
            act(view("LH", 4 * k + 2 * j, 4 * k + 2 * j + 2), view("PC"), bias=2.0 * m * (E * r + j), scale=2.0 * m)
    act(view("I0", 0, 1), view("PC", 0, 1), bias=-254.0 * E * r - 256.0 - 2.0 * P * r, scale=-254.0)
    act(view("P2"), view("PC"), bias=2.0 * E * r - 128.0 - 2.0 * P * r, scale=2.0)
    act(view("PN"), view("PC"), bias=2.0 * E * r - 128.0 - 2.0 * P * (r + 1), scale=2.0)
    act(view("H2"), view("PF"), bias=2.0 * MA * E * r, scale=2.0 * MA)
    ts(view("H4"), view("WC", 0, 8, step=2), view("H2"), ADD)
    act(view("NH"), view("PF"), bias=-2.0 * MA * (E * r + 1), scale=-2.0 * MA)
    act(view("WH", 128, 129), view("PF"), bias=4.0 * E * r - 256.0, scale=4.0)
    if r == 0:
        fill(view("W", 128, 528, step=264), 0.0)
    if r == N - 1:
        fill(view("W", 260, 528, step=264), 0.0)

    sc, mc = view("EX2", 8, 9, 0, 96), view("EX2", 144, 145, 0, 96)
    for k, row in ((0, "DS"), (1, "DN")):
        c = 136 * k + 8
        scan(view("EX2", c - 7, c + 32), view("X2L", 2 + k, 80 + k, step=2), view("X2L", 18, 57))
        turn(view(row, 0, 32, 0, 96), view("EX2", c, c + 32, 0, 96))
        for a in (0, 2):
            turn(quarter(row, a, 32, 64), quarter("EX2", 2 - a, c, c + 32))
            copy(quarter(row, a, 64, 96), quarter(row, 1, 0, 32))
        copy(quarter(row, 1, 32, 96), quarter(row, 0, 0, 64))
    ds, dn, sg, lo, bf = [view(x, 0, 96, 0, 96) for x in ("DS", "DN", "SG", "LO", "BF")]
    act(sg, ds, AF.Sign, sc, -1.0)
    ts(lo, dn, mc, GE, -0.5, MUL)
    tt(bf, sg, lo, LE)
    fill(view("BF", 96, 135), 0.0)
    fill(view("EX2", 41, 137), -HUGE)
    scan(view("EXM", 0, 135, 0, 96), view("BF", 0, 135, 0, 96), view("EX2", 41, 176, 0, 96), 0.5 - K, MAX)
    ts(quarter("EXM", 3, 103, 135), quarter("EX2", 0, 144, 176), UNIT, ADD)
    turn(view("MR", 0, 32), view("EXM", 103, 135))
    for h in (0, 1):
        turn(half("MR", h, 32, 64), half("EXM", 1 - h, 103, 135))
    swap("MR", 32)
    signs(view("MR"), view("EXM", 134, 135), view("RK"), -1.0)
    for k, m in ((0, MA), (1, MB)):
        ts(view("F0", k, k + 1), view("EXM", 134, 135), 0.5 / UNIT * m, MUL, view("FC", k, k + 1), ADD)
    if r > 0:
        signs(view("MR"), (4.0 * P * r - 0.5) * UNIT, view("SB", 0, 1), -1.0)
    if r < N - 1:
        signs(view("MR"), (4.0 * P * (r + 1) - 0.5) * UNIT, view("SB", 1, 2), -1.0)
    for k, row in ((0, "FR"), (1, "FB")):
        lay(view("EXF", 64 * k, 64 * k + 32), view("KK", 32 * k, 32 * k + 32), view("RK"), view("F0", k, k + 1))
        for h in (0, 1):
            lay(half("EXF", h, 64 * k + 32, 64 * k + 64), half("KK", 1 - h, 32 * k, 32 * k + 32), half("RK", 1 - h), half("F0", 1 - h, k, k + 1))
        turn(view(row, 0, 64), view("EXF", 64 * k, 64 * k + 64))
        swap(row, 32)

    if r > 0:
        ts(view("W", 128, 528, step=264), view("P2"), view("SB", 0, 1), LT, 2.0 * cut, MUL, "low")
    if r < N - 1:
        ts(view("W", 260, 528, step=264), view("PN"), view("SB", 1, 2), GE, -2.0 * (H0 - 32 - 8 * r), MUL, "high")
    for h in range(2):
        for k, row in ((0, "FR"), (1, "FB")):
            c = 264 * h + 132 * k
            if h + k < 2:
                ts(view("W", c, c + 128), view(row), view("LH", 4 * k + h, 4 * k + h + 1), MAX, view("LH", 4 * k + 2 + h, 4 * k + 3 + h), MIN)
            else:
                ts(view("W", c + 1, c + 128), view("ZB", 1, 128), view("LH", 1, 2), ADD)
                act(view("W", c, c + 1), view("PC", 1, 2), bias=2.0 * MB * E * r + 256.0 + 2.0 * P * r + 256.0 * MB, scale=2.0 * MB)
                act(view("NL"), view("PC", 1, 2), bias=-2.0 * MB * E * r, scale=-2.0 * MB)
                act(view("TW"), view(row), AF.Relu, view("NL"))
                act(waste(view("TW")), view("TW"), AF.Relu, 2.0 * MB, -1.0, view("I0", 1, 2), "I1")
        scan(view("OF", 130 * h, 130 * h + 129), view("W", 264 * h, 264 * h + 129), view("W", 264 * h + 132, 264 * h + 261), view("I0", h, h + 1), SUB)
    for a in range(4):
        for b in (a, a ^ 1):
            copy(quarter("OTF", b, 2 * a, 2 * a + 2), quarter("OF", a, 128, 260, 130))
    for d in (0, 1):
        for h in (0, 1):
            ts(half("OT", d, 4 * h, 4 * h + 4), half("OTF", h, 4 * h, 4 * h + 4), 0.5, MUL)
    op("v", lambda e, q: e.tensor_copy(T.RUN[:, 0:128].bitcast(dt.uint32), T.SRC[:, 0:ALL].bitcast(dt.uint32).indirect(T.OT[:, 0:8])),
       [view("SRC"), view("OT")], [view("RUN")])
    op("vs", lambda e, q: e.activation(T.sRUN[:, 0:128], T.sSRC[:, 0:ALL].indirect(T.OT[:, 0:8]), AF.Copy) if q == "s"
       else e.tensor_copy(T.sRUN[:, 0:128], T.sSRC[:, 0:ALL].indirect(T.OT[:, 0:8])), [view("sSRC"), view("OT")], [view("sRUN")])

    op("vs", lambda e, q: e.tensor_copy(T.YT[:], T.YS[:].indirect(T.OT[:, 0:8])) if q == "v"
       else e.activation(T.YT[:], T.YS[:].indirect(T.OT[:, 0:8]), AF.Copy), [view("YS"), view("OT")], [view("YT")])
    store(lambda e: e.dma_start(T.y[:, 0:E], T.YT[:, 0:E]), view("YT"), "o5")
    store(lambda e: e.dma_start(T.oc[:, 0:4 * E], T.RUN[:, 0:E].bitcast(dt.uint8)), view("RUN", 0, E), "o0")
    for k in range(4):
        store(lambda e, k=k: e.dma_start(T.osc[4 * k:4 * k + 4, 0:E], T.sRUN[32 * k:32 * k + 4, 0:E]), view("sRUN", 0, E, 32 * k, 32 * k + 4), "o%d" % (1 + k))
    for k in (129, 130):
        signs(view("FR"), view("NH"), view("WH", k, k + 1))
    for k in range(4):
        ts(view("WH", 32 * k, 32 * k + 32), view("FR", 32 * k, 32 * k + 32), view("H4", k, k + 1), EQ, view("WC", 2 * k + 1, 2 * k + 2), MUL)
    sums(view("HB"), view("WH", 0, 131))
    store(lambda e: e.dma_start(T.hs[0:1, 0:E], T.HB[0:E, 0:1]), view("HB", 0, 1, 0, E), "o6")

    order, queue = place(ops, *links(ops), ORDER)
    total, known, clocks, log = {}, {k: {} for k in queues}, {}, {}

    def await_(q, need):
        for s, n in sorted(need.items()):
            if known[q].get(s, 0) < n:
                queues[q].wait_ge(T.sem[s], n)
                for s2, n2 in clocks.get((s, n), {}).items():
                    known[q][s2] = max(known[q].get(s2, 0), n2)
                known[q][s] = n

    for i in order:
        o, q = ops[i], queue[i]
        sem = o["sem"] or q
        if o["fn"] is not None:
            need = {}
            for w, wr in accesses(o):
                for v, vr, s, n, q2 in log.get(w[0], []):
                    if (wr or vr or (w[0] == "ps" and q2 != q)) and meet(wide(w), v):
                        need[s] = max(need.get(s, 0), n)
            await_(q, need)
            ins = o["fn"](queues[q], q)
            if o["local"]:
                ins.then_inc(T.sem[sem], o["inc"])
            total[sem] = total.get(sem, 0) + o["inc"]
            clocks[(sem, total[sem])] = dict(known[q])
        else:
            total[sem] = o["inc"]
        for w, wr in accesses(o):
            w = wide(w)
            l = log.setdefault(w[0], [])
            if wr:
                l[:] = [e for e in l if not holds(w, e[0])]
            l.append((w, wr, sem, total[sem], q))
    await_("y", total)
